import numpy as np
import ml_dtypes


def mxq(x, axis, fmt="e4m3"):
    dtype, down = {"e4m3": (ml_dtypes.float8_e4m3fn, 7), "e5m2": (ml_dtypes.float8_e5m2, 14)}[fmt]
    v = np.moveaxis(np.asarray(x, np.float32).astype(ml_dtypes.bfloat16).astype(np.float64), axis, -1)
    blocks = v.reshape(v.shape[:-1] + (-1, 32))
    amax = np.abs(blocks).max(-1, keepdims=True)
    byte = np.maximum(np.where(amax > 0, np.frexp(amax)[1] - 1 + 127, 0) - down, 1)
    scale = np.exp2(byte - 127.0)
    codes = (blocks / scale).astype(np.float32).astype(dtype).astype(np.float64)
    return np.moveaxis((codes * scale).reshape(v.shape), -1, axis)


WIDE = False


def mx_kscale(k):
    if not WIDE:
        return np.ones(k)
    levels = np.array([30, -30])
    if k % 512:
        return np.exp2(np.random.permutation(np.resize(levels, k // 32))).repeat(32)
    a = np.empty((k // 512, 16))
    for p in range(k // 512):
        a[p, :8] = np.random.permutation(np.resize(levels, 8))
        for g in range(8):
            far = levels[np.abs(levels - a[p, g]) >= 10]
            a[p, g + 8] = far[np.random.randint(len(far))]
    return np.exp2(a.ravel()).repeat(32)


BF16 = ml_dtypes.bfloat16


def bf(x):
    return np.asarray(x, np.float32).astype(BF16)


def f64(x):
    return np.asarray(x).astype(np.float64)


T, D, F = 1024, 512, 1536


def setup_inputs():
    s = mx_kscale(D)
    t = mx_kscale(T)
    r = mx_kscale(F)
    return {"dy": bf(np.random.standard_normal((T, D)) * s),
            "wo": bf(np.random.standard_normal((F, D)) / np.sqrt(D) / s),
            "u": bf(np.random.standard_normal((T, F)) * t[:, None] * r),
            "f": bf(1 + 0.5 * np.random.standard_normal((T, F))),
            "n": bf(np.random.standard_normal((T, F))),
            "gamma": bf((1 + 0.1 * np.random.standard_normal(F)) / r),
            "beta": bf(0.3 * np.random.standard_normal(F) / r),
            "ws": bf(np.random.standard_normal((T, T)) / np.sqrt(T) / t[:, None]),
            "eta": bf((1 + 0.1 * np.random.standard_normal(T)) / np.sqrt(F) / t)}


def reference(dy, wo, u, f, n, gamma, beta, ws, eta):
    dg = mxq(f64(dy), 1, "e4m3") @ mxq(f64(wo), 1, "e4m3").T
    du = dg * f64(f)
    df = dg * f64(u)
    dv = mxq(f64(ws), 0, "e4m3").T @ mxq(df, 0, "e5m2")
    dn = dv * f64(gamma)
    v = f64(n) * f64(gamma) + f64(beta)
    dws = mxq(df, 1, "e5m2") @ mxq(v, 1, "e4m3").T
    step = dws * f64(eta)[:, None]
    return du, dn, step

@@ -1,0 +1,477 @@
+from contextlib import ExitStack
+
+import concourse.mybir as mybir
+from concourse.masks import make_identity
+
+T, D, F = 1024, 512, 1536
+FLOPS = 2 * T * D * F + 4 * T * T * F
+
+F32 = mybir.dt.float32
+BF16 = mybir.dt.bfloat16
+U32 = mybir.dt.uint32
+U8 = mybir.dt.uint8
+E4 = mybir.dt.float8_e4m3fn_x4
+E5 = mybir.dt.float8_e5m2_x4
+ACT = mybir.ActivationFunctionType
+MULT = mybir.AluOpType.mult
+
+P = 128
+W = 512
+UNITS = [(h, g) for h in range(2) for g in range(3)]
+RAW_SLOTS = 18
+WS_ENGINE = "s"
+V_ENGINES = "vvssvs"
+OUT_SLOTS = 6
+
+
+def tile_gmlp_gating_backward_f3_kernel(tc, dy, wo, u, f, n, gamma, beta, ws, eta, out_0, out_1, out_2):
+    nc = tc.nc
+    with ExitStack() as ctx:
+        sb = ctx.enter_context(tc.tile_pool(name="sb", bufs=1))
+        ps = ctx.enter_context(tc.psum_pool(name="ps", bufs=1))
+        turns = {}
+
+        def ring(pool, name, slots, shape, dtype):
+            k = turns.get(name, 0)
+            turns[name] = k + 1
+            tag = "%s%d" % (name, k % slots)
+            return pool.tile(shape, dtype, name=tag, tag=tag, align_bytes=64)
+
+        def new_bank(name):
+            tags = role[name]
+            k = turns.get(tags, 0)
+            turns[tags] = k + 1
+            tag = "bank%d" % tags[k % len(tags)]
+            return ps.tile([P, W], F32, name=tag, tag=tag)
+
+        role = {"dg": (0, 1, 2), "tr": (3, 4, 5, 6, 7), "acc": (5, 6, 7)}
+
+        ident = sb.tile([P, P], F32, name="ident")
+        make_identity(nc, ident[:])
+        ctx.enter_context(tc.manual_schedule(engines={mybir.EngineType.SP}))
+
+        raw = {}
+
+        def load(key, src):
+            raw[key] = ring(sb, "raw", RAW_SLOTS, [P, 4, W], BF16)
+            nc.sync.dma_start(out=raw[key][:], in_=src)
+
+        def rows4(x, h, g):
+            return x[h * W:(h + 1) * W, g * W:(g + 1) * W].rearrange("(p t) c -> p t c", t=4)
+
+        def load_dy(h):
+            load(("dy", h), rows4(dy, h, 0))
+
+        def load_wo(g):
+            load(("wo", g), wo[g * W:(g + 1) * W, :].rearrange("(b m) k -> m b k", b=4))
+
+        def load_unit(i):
+            h, g = UNITS[i]
+            load(("u", i), rows4(u, h, g))
+            load(("f", i), rows4(f, h, g))
+
+        def load_ws(h, jh):
+            load(("ws", h, jh), rows4(ws, h, jh))
+
+        def load_n(g, jh):
+            load(("n", g, jh), rows4(n, jh, g))
+
+        codes = {}
+        staged = {}
+
+        def quantize(key, fmt, name, slots, part=0, parts=1):
+            if part == 0:
+                codes[key] = (ring(sb, name + "c", slots, [P, W], U32), ring(sb, name + "s", slots, [P, W], U8))
+            width = W // parts
+            cols = slice(part * width, (part + 1) * width)
+            nc.vector.quantize_mx(
+                out=codes[key][0][:, cols].bitcast(fmt),
+                scales=codes[key][1][:, cols],
+                in_=staged[key][:, 4 * part * width:4 * (part + 1) * width],
+            )
+
+        def mm(bank, lhs_key, lhs_fmt, lhs_cols, rhs_key, rhs_fmt, rhs_cols, start, stop):
+            nc.tensor.matmul_mx(
+                out=bank,
+                lhsT=codes[lhs_key][0][:, lhs_cols].bitcast(lhs_fmt),
+                lhsT_scale=codes[lhs_key][1][:, lhs_cols],
+                rhs=codes[rhs_key][0][:, rhs_cols].bitcast(rhs_fmt),
+                rhs_scale=codes[rhs_key][1][:, rhs_cols],
+                start=start,
+                stop=stop,
+            )
+
+        def block(j):
+            return slice(j * P, (j + 1) * P)
+
+        def turn_half(key, half, engine):
+            if half == 0:
+                staged[key] = ring(sb, "grp", 3, [P, 4 * W], BF16)
+            if key in raw:
+                rows = raw[key][:, 2 * half:2 * half + 2, :]
+            else:
+                rows = raw[key + (half,)][:]
+            words = rows.rearrange("p a k -> p (a k)").bitcast(F32)
+            bank = new_bank("tr")
+            for a in range(2):
+                for w in range(2):
+                    nc.tensor.transpose(bank[:, block(2 * a + w)], words[:, 256 * a + w:256 * (a + 1):2], ident[:])
+            src = bank[:].rearrange("p (a w m) -> p a m w", a=2, w=2)
+            out = staged[key][:].bitcast(F32)[:, half * W:(half + 1) * W].rearrange("p (a m w) -> p a m w", a=2, w=2)
+            if engine == "s":
+                nc.scalar.copy(out=out, in_=src)
+            else:
+                nc.vector.tensor_copy(out=out, in_=src)
+
+        def turn_input(key):
+            turn_half(key, 0, "s")
+            turn_half(key, 1, "s")
+
+        def interleave(key, src, engine):
+            staged[key] = ring(sb, "grp", 3, [P, 4 * W], BF16)
+            out = staged[key][:].rearrange("p (c i t) -> p c t i", i=4, t=4)
+            in_ = src[:].rearrange("p t (c i) -> p c t i", i=4)
+            if engine == "s":
+                nc.scalar.copy(out=out, in_=in_)
+            elif engine == "v":
+                nc.vector.tensor_copy(out=out, in_=in_)
+            else:
+                out = staged[key][:].rearrange("p (c t) -> p c t", t=4)
+                in_ = src[:].rearrange("p t c -> p c t")
+                for j in range(4):
+                    nc.gpsimd.tensor_scalar(out=out[:, block(j), :], in0=in_[:, block(j), :], scalar1=1.0, scalar2=0.0, op0=MULT, op1=mybir.AluOpType.add)
+
+        dg_banks = {}
+        outs = {}
+
+        def dg(i):
+            h, g = UNITS[i // 4]
+            bank = new_bank("dg")
+            dg_banks[i] = bank
+            for t in range(4):
+                mm(bank[:, block(t)], ("dy", h), E4, block(t), ("wo", g), E4, block(i % 4), True, True)
+
+        def df(i):
+            un, b = divmod(i, 4)
+            if b == 0:
+                staged[("a", un)] = ring(sb, "dfa", 2, [P, 4 * W], BF16)
+            out = staged[("a", un)][:].rearrange("p (s q t) -> p q t s", s=4, t=4)[:, 32 * b:32 * (b + 1), :, :]
+            nc.vector.tensor_tensor(
+                out=out,
+                in0=dg_banks[i][:].rearrange("p (t q s) -> p q t s", t=4, s=4),
+                in1=raw[("u", un)][:, :, block(b)].rearrange("p t (q s) -> p q t s", s=4),
+                op=MULT,
+            )
+
+        def du(i):
+            un, b = divmod(i, 4)
+            if b == 0:
+                outs[("du", un)] = ring(sb, "out", OUT_SLOTS, [P, 4, W], F32)
+            nc.vector.tensor_tensor(
+                out=outs[("du", un)][:, :, block(b)],
+                in0=dg_banks[i][:].rearrange("p (t c) -> p t c", t=4),
+                in1=raw[("f", un)][:, :, block(b)],
+                op=MULT,
+            )
+
+        def store_du(un):
+            h, g = UNITS[un]
+            nc.sync.dma_start(out=rows4(out_0, h, g), in_=outs[("du", un)][:])
+
+        def turn_df(un, halves=range(2)):
+            if halves[0] == 0:
+                staged[("b", un)] = ring(sb, "dfb", 2, [P, 4 * W], BF16)
+            words = staged[("a", un)][:].bitcast(F32)
+            for w in halves:
+                bank = new_bank("tr")
+                for s in range(4):
+                    nc.tensor.transpose(bank[:, block(s)], words[:, 256 * s + w:256 * (s + 1):2], ident[:])
+                nc.scalar.copy(
+                    out=staged[("b", un)][:, w * 2 * W:(w + 1) * 2 * W].rearrange("p (e m s) -> p e m s", e=2, s=4),
+                    in_=bank[:].bitcast(BF16).rearrange("p (s m e) -> p e m s", s=4, e=2),
+                )
+
+        vs = {}
+
+        def make_v(g, jh, word_halves=range(2)):
+            if word_halves[0] == 0:
+                vs[(g, jh)] = ring(sb, "vs", 2, [P, 4, W], BF16)
+            words = raw[("n", g, jh)][:].rearrange("p a c -> p (a c)").bitcast(F32)
+            for w in word_halves:
+                bank = new_bank("tr")
+                for a in range(4):
+                    nc.tensor.transpose(bank[:, block(a)], words[:, 256 * a + w:256 * (a + 1):2], ident[:])
+                halves = bank[:].bitcast(BF16).rearrange("p (a m e) -> p e m a", a=4, e=2)
+                for e in range(2):
+                    s = 2 * w + e
+                    nc.scalar.activation(
+                        out=vs[(g, jh)][:, s, :].rearrange("p (m a) -> p m a", a=4),
+                        in_=halves[:, e, :, :],
+                        func=ACT.Identity,
+                        scale=gam[:, 4 * g + s:4 * g + s + 1],
+                        bias=bet[:, 4 * g + s:4 * g + s + 1],
+                    )
+
+        def spread_gamma(g):
+            bank = new_bank("tr")
+            for s in range(4):
+                nc.tensor.transpose(bank[:, block(s)], gam[:, 4 * g + s:4 * g + s + 1].to_broadcast([P, P]), ident[:])
+            nc.scalar.copy(
+                out=gam_rows[:, g * W:(g + 1) * W].rearrange("p (q s) -> p q s", s=4),
+                in_=bank[:].rearrange("p (s q) -> p q s", s=4),
+            )
+
+        acc = {}
+
+        def dv(g, jt, role_name="acc"):
+            bank = new_bank(role_name)
+            acc[("dv", g, jt)] = bank
+            for h in range(2):
+                mm(bank[:], ("ws", h, jt // 4), E4, block(jt % 4), ("a", UNITS.index((h, g))), E5, slice(0, W), h == 0, h == 1)
+
+        def dn(g, jt):
+            if jt % 4 == 0:
+                outs[("dn", g, jt // 4)] = ring(sb, "out", OUT_SLOTS, [P, 4, W], F32)
+            nc.vector.tensor_tensor(
+                out=outs[("dn", g, jt // 4)][:, jt % 4, :].rearrange("p (q s) -> p q s", s=4),
+                in0=acc[("dv", g, jt)][:].rearrange("p (s q) -> p q s", s=4),
+                in1=gam_rows[:, g * W:(g + 1) * W].rearrange("p (q s) -> p q s", s=4),
+                op=MULT,
+            )
+
+        def store_dn(g, jh, bs=slice(0, 4)):
+            dst = out_1[jh * W:(jh + 1) * W, g * W:(g + 1) * W].rearrange("(b p) c -> p b c", b=4)
+            nc.sync.dma_start(out=dst[:, bs, :], in_=outs[("dn", g, jh)][:, bs, :])
+
+        def dws(h, k, groups=range(3), role_name="acc"):
+            jh, t = divmod(k, 4)
+            if groups[0] == 0:
+                acc[("dws", h, k)] = new_bank(role_name)
+            bank = acc[("dws", h, k)]
+            for g in groups:
+                mm(bank[:], ("b", UNITS.index((h, g))), E5, block(t), ("v", g, jh), E4, slice(0, W), g == 0, g == 2)
+
+        def step(h, k):
+            jh, t = divmod(k, 4)
+            if t == 0:
+                outs[("step", h, jh)] = ring(sb, "out", OUT_SLOTS, [P, 4, W], F32)
+            nc.scalar.activation(
+                out=outs[("step", h, jh)][:, t, :],
+                in_=acc[("dws", h, k)][:],
+                func=ACT.Copy,
+                scale=eta32[:, 4 * h + t:4 * h + t + 1],
+            )
+
+        def store_step(h, jh, ts):
+            nc.sync.dma_start(out=rows4(out_2, h, jh)[:, ts, :], in_=outs[("step", h, jh)][:, ts, :])
+
+        gam16 = sb.tile([P, 3, 4], BF16, name="gam16")
+        bet16 = sb.tile([P, 3, 4], BF16, name="bet16")
+        eta16 = sb.tile([P, 2, 4], BF16, name="eta16")
+        gam = sb.tile([P, 12], F32, name="gam")
+        bet = sb.tile([P, 12], F32, name="bet")
+        eta32 = sb.tile([P, 8], F32, name="eta32")
+        gam_rows = sb.tile([P, F], BF16, name="gam_rows")
+
+        def load_half(key, half, src):
+            raw[key + (half,)] = ring(sb, "first", 4, [P, 2, W], BF16)
+            nc.sync.dma_start(out=raw[key + (half,)][:], in_=src[:, 2 * half:2 * half + 2, :])
+
+        dy_first = rows4(dy, 0, 0)
+        wo_first = wo[0:W, :].rearrange("(b m) k -> m b k", b=4)
+        load_half(("dy", 0), 0, dy_first)
+        load_half(("wo", 0), 0, wo_first)
+        load_half(("dy", 0), 1, dy_first)
+        nc.scalar.dma_start(out=gam16[:], in_=gamma.rearrange("(g q s) -> q g s", g=3, s=4))
+        nc.scalar.dma_start(out=bet16[:], in_=beta.rearrange("(g q s) -> q g s", g=3, s=4))
+        load(("u", 0), rows4(u, 0, 0))
+        load_half(("wo", 0), 1, wo_first)
+        load(("f", 0), rows4(f, 0, 0))
+        load_n(0, 0)
+        load_wo(1)
+        load_unit(1)
+        load_n(1, 0)
+        load_wo(2)
+        nc.sync.dma_start(out=eta16[:], in_=eta.rearrange("(h p t) -> p h t", h=2, t=4))
+        load_n(2, 0)
+        load_unit(2)
+        load_dy(1)
+        load_unit(3)
+        load_ws(0, 0)
+        load_ws(1, 0)
+        load_ws(0, 1)
+        load_ws(1, 1)
+
+        nc.scalar.activation(out=gam[:], in_=gam16[:].rearrange("p g s -> p (g s)"), func=ACT.Identity)
+        turn_half(("dy", 0), 0, "s")
+        turn_half(("wo", 0), 0, "v")
+        turn_half(("dy", 0), 1, "s")
+        quantize(("dy", 0), E4, "dyq", 2, 0, 2)
+        quantize(("wo", 0), E4, "woq", 3, 0, 2)
+        quantize(("dy", 0), E4, "dyq", 2, 1, 2)
+        turn_half(("wo", 0), 1, "s")
+        nc.scalar.activation(out=bet[:], in_=bet16[:].rearrange("p g s -> p (g s)"), func=ACT.Identity)
+        dg(0)
+        dg(1)
+        for g in range(3):
+            spread_gamma(g)
+
+        def q_dy(h):
+            quantize(("dy", h), E4, "dyq", 2)
+
+        def q_wo(g):
+            quantize(("wo", g), E4, "woq", 3)
+
+        def q_ws(h, jh):
+            quantize(("ws", h, jh), E4, "wsq", 4)
+
+        def q_v(g, jh):
+            quantize(("v", g, jh), E4, "vq", 6)
+
+        def q_a(un):
+            quantize(("a", un), E5, "aq", 5)
+
+        def q_b(un):
+            quantize(("b", un), E5, "bq", 5)
+
+        def il_ws(h, jh):
+            interleave(("ws", h, jh), raw[("ws", h, jh)], WS_ENGINE)
+
+        def il_v(g, jh):
+            interleave(("v", g, jh), vs[(g, jh)], V_ENGINES[3 * jh + g])
+
+        def eta_f32():
+            nc.scalar.activation(out=eta32[:], in_=eta16[:].rearrange("p h t -> p (h t)"), func=ACT.Identity)
+
+        def late_loads():
+            load_unit(4)
+            for g in range(3):
+                load_n(g, 1)
+            load_unit(5)
+
+        def narrow_tr():
+            role["tr"] = (3, 4)
+
+        plan = {(i, where): [] for i in range(24) for where in range(4)}
+
+        def at(i, where, fn, *args):
+            plan[(i, where)].append((fn, args))
+
+        def run(i, where):
+            for fn, args in plan[(i, where)]:
+                fn(*args)
+
+        dg_step = {j: j - 2 if j >= 2 else -1 for j in range(24)}
+        dg_step[2] = 1
+        dg_step[4] = 3
+        first, second = range(0, 1), range(1, 2)
+        at(0, 3, quantize, ("wo", 0), E4, "woq", 3, 1, 2)
+        at(1, 1, make_v, 0, 0, first)
+        at(1, 1, turn_input, ("wo", 1))
+        at(1, 1, make_v, 0, 0, second)
+        at(2, 3, q_wo, 1)
+        for un in range(5):
+            at(4 * un + 4, 2, q_a, un)
+        at(4, 1, turn_df, 0)
+        at(4, 1, turn_input, ("wo", 2))
+        at(4, 3, il_v, 0, 0)
+        at(5, 0, make_v, 1, 0)
+        at(5, 3, q_v, 0, 0)
+        at(5, 3, q_wo, 2)
+        at(6, 3, q_b, 0)
+        at(7, 0, make_v, 2, 0)
+        at(7, 3, il_v, 1, 0)
+        at(7, 3, late_loads)
+        at(7, 3, store_du, 0)
+        at(7, 3, store_du, 1)
+        for un in range(2, 5):
+            at(4 * un + 3, 3, store_du, un)
+        at(8, 1, turn_input, ("dy", 1))
+        at(8, 1, turn_df, 1)
+        at(8, 3, q_v, 1, 0)
+        at(9, 1, eta_f32)
+        at(9, 1, il_v, 2, 0)
+        at(9, 3, q_dy, 1)
+        at(11, 3, q_b, 1)
+        at(12, 1, turn_df, 2)
+        at(12, 3, q_v, 2, 0)
+        at(12, 3, narrow_tr)
+        at(12, 3, il_ws, 0, 0)
+        at(14, 3, q_b, 2)
+        for k in range(4):
+            at(15, 1, dws, 0, k)
+            at(15, 1, step, 0, k)
+        at(15, 3, store_step, 0, 0, slice(0, 4))
+        at(15, 0, il_ws, 1, 0)
+        at(15, 3, q_ws, 0, 0)
+        at(16, 3, q_ws, 1, 0)
+        at(16, 1, turn_df, 3)
+        at(16, 1, il_ws, 0, 1)
+        at(17, 0, il_ws, 1, 1)
+        at(18, 0, make_v, 0, 1)
+        at(18, 3, q_ws, 0, 1)
+        at(18, 3, q_b, 3)
+        at(19, 0, make_v, 1, 1)
+        at(19, 1, q_ws, 1, 1)
+        at(20, 1, il_v, 0, 1)
+        at(20, 1, turn_df, 4)
+        at(20, 3, il_v, 1, 1)
+        at(21, 0, make_v, 2, 1)
+        at(21, 0, il_v, 2, 1)
+        at(21, 3, q_v, 0, 1)
+        at(21, 3, q_v, 1, 1)
+        at(22, 1, q_b, 4)
+        at(22, 1, q_v, 2, 1)
+        jobs = [(dv, dn, 0, jt) for jt in range(8)] + [(dv, dn, 1, jt) for jt in range(8)] + [(dws, step, 0, k) for k in range(4, 8)]
+        slots = [(17, 2), (17, 3), (18, 1), (18, 2), (19, 2), (19, 3), (20, 3), (20, 3), (21, 1), (21, 1), (21, 2), (21, 3), (22, 1), (22, 2), (22, 3), (22, 3), (23, 1), (23, 1), (23, 1), (23, 1)]
+        make_slots = [(17, 1), (17, 1)] + slots[:-2]
+        make_slots[4:6] = [(19, 1), (19, 1)]
+        for k, (make, read, x, y) in enumerate(jobs):
+            at(*make_slots[k], make, x, y)
+            if k >= 2:
+                make, read, x, y = jobs[k - 2]
+                at(*slots[k - 2], read, x, y)
+                if y % 4 == 3:
+                    at(*slots[k - 2], store_dn if read is dn else store_step, x, y // 4, slice(0, 4))
+        at(23, 1, step, 0, 6)
+        at(23, 1, step, 0, 7)
+        at(23, 1, store_step, 0, 1, slice(0, 4))
+
+        for i in range(24):
+            run(i, 0)
+            for j in range(24):
+                if dg_step[j] == i:
+                    dg(j)
+            run(i, 1)
+            df(i)
+            run(i, 2)
+            if i < 21:
+                du(i)
+            run(i, 3)
+
+        for k in range(3):
+            dws(1, k, range(2))
+        turn_df(5)
+        q_a(5)
+        role["tail"] = (0, 1, 2, 3, 4)
+        for jt in range(3):
+            du(21 + jt)
+            dv(2, jt, "tail")
+        store_du(5)
+        q_b(5)
+        dv(2, 3, "tail")
+        dv(2, 4, "tail")
+        for jt in range(8):
+            dn(2, jt)
+            if jt < 3:
+                dv(2, 5 + jt, "tail")
+                dws(1, jt, range(2, 3))
+                step(1, jt)
+            if jt % 2 == 1:
+                store_dn(2, jt // 4, slice(jt % 4 - 1, jt % 4 + 1))
+        store_step(1, 0, slice(0, 2))
+        for k in range(3, 8):
+            dws(1, k)
+            step(1, k)
+            if k % 2 == 1:
+                store_step(1, k // 4, slice(k % 4 - 1, k % 4 + 1))

@@ -18,10 +18,12 @@ MULT = mybir.AluOpType.mult
 P = 128
 W = 512
 UNITS = [(h, g) for h in range(2) for g in range(3)]
-RAW_SLOTS = 18
-WS_ENGINE = "s"
-V_ENGINES = "vvssvs"
-OUT_SLOTS = 6
+DIRECT = False
+TWICE = 0
+WS_ENGINES = "ssss"
+V_ENGINES = "ssssss"
+A_ENGINES = "vvvvvv"
+G_PARTS = 4
 
 
 def tile_gmlp_gating_backward_f3_kernel(tc, dy, wo, u, f, n, gamma, beta, ws, eta, out_0, out_1, out_2):
@@ -31,11 +33,19 @@ def tile_gmlp_gating_backward_f3_kernel(tc, dy, wo, u, f, n, gamma, beta, ws, et
         ps = ctx.enter_context(tc.psum_pool(name="ps", bufs=1))
         turns = {}
 
-        def ring(pool, name, slots, shape, dtype):
+        def slot(tag, shape, dtype):
+            return sb.tile(shape, dtype, name=tag, tag=tag, align_bytes=64)
+
+        def ring(name, slots, shape, dtype):
             k = turns.get(name, 0)
             turns[name] = k + 1
-            tag = "%s%d" % (name, k % slots)
-            return pool.tile(shape, dtype, name=tag, tag=tag, align_bytes=64)
+            return slot("%s%d" % (name, k % slots), shape, dtype)
+
+        def out_tile():
+            tags = ["out0", "out1", "out2", "u_wide0", "f_wide0", "n_wide0"]
+            k = turns.get("out", 0)
+            turns["out"] = k + 1
+            return slot(tags[k % len(tags)], [P, 4, W], F32)
 
         def new_bank(name):
             tags = role[name]
@@ -48,40 +58,47 @@ def tile_gmlp_gating_backward_f3_kernel(tc, dy, wo, u, f, n, gamma, beta, ws, et
 
         ident = sb.tile([P, P], F32, name="ident")
         make_identity(nc, ident[:])
-        ctx.enter_context(tc.manual_schedule(engines={mybir.EngineType.SP}))
 
         raw = {}
 
-        def load(key, src):
-            raw[key] = ring(sb, "raw", RAW_SLOTS, [P, 4, W], BF16)
-            nc.sync.dma_start(out=raw[key][:], in_=src)
+        def rows4(x, h, g, groups=1):
+            return x[h * W:(h + 1) * W, g * W:(g + groups) * W].rearrange("(p t) c -> p t c", t=4)
 
-        def rows4(x, h, g):
-            return x[h * W:(h + 1) * W, g * W:(g + 1) * W].rearrange("(p t) c -> p t c", t=4)
+        def load(name, x, h, g, groups):
+            tile = slot("%s_%s%d" % (name, "wide" if groups > 1 else "one", h), [P, 4, groups * W], BF16)
+            nc.sync.dma_start(out=tile[:], in_=rows4(x, h, g, groups))
+            for j in range(groups):
+                raw[(name, h, g + j)] = (tile, j)
 
-        def load_dy(h):
-            load(("dy", h), rows4(dy, h, 0))
+        def piece(key):
+            tile, j = raw[key]
+            return tile[:, :, j * W:(j + 1) * W]
+
+        def word_columns(source, a, w):
+            tile, j = source
+            width = tile.shape[2] // 2
+            base = a * width + j * 256
+            return tile[:].rearrange("p a c -> p (a c)").bitcast(F32)[:, base + w:base + 256:2]
+
+        def wo_rows(g):
+            return wo[g * W:(g + 1) * W, :].rearrange("(b m) k -> m b k", b=4)
 
         def load_wo(g):
-            load(("wo", g), wo[g * W:(g + 1) * W, :].rearrange("(b m) k -> m b k", b=4))
+            tile = slot("wo%d" % g, [P, 4, W], BF16)
+            nc.sync.dma_start(out=tile[:], in_=wo_rows(g))
+            raw[("wo", g)] = (tile, 0)
 
-        def load_unit(i):
-            h, g = UNITS[i]
-            load(("u", i), rows4(u, h, g))
-            load(("f", i), rows4(f, h, g))
-
-        def load_ws(h, jh):
-            load(("ws", h, jh), rows4(ws, h, jh))
-
-        def load_n(g, jh):
-            load(("n", g, jh), rows4(n, jh, g))
+        def load_half(key, half, src):
+            tile = ring("first", 4, [P, 2, W], BF16)
+            nc.sync.dma_start(out=tile[:], in_=src[:, 2 * half:2 * half + 2, :])
+            raw[key + (half,)] = (tile, 0)
 
         codes = {}
         staged = {}
 
         def quantize(key, fmt, name, slots, part=0, parts=1):
             if part == 0:
-                codes[key] = (ring(sb, name + "c", slots, [P, W], U32), ring(sb, name + "s", slots, [P, W], U8))
+                codes[key] = (ring(name + "c", slots, [P, W], U32), ring(name + "s", slots, [P, W], U8))
             width = W // parts
             cols = slice(part * width, (part + 1) * width)
             nc.vector.quantize_mx(
@@ -104,18 +121,22 @@ def tile_gmlp_gating_backward_f3_kernel(tc, dy, wo, u, f, n, gamma, beta, ws, et
         def block(j):
             return slice(j * P, (j + 1) * P)
 
-        def turn_half(key, half, engine):
+        def new_staged(key):
+            staged[key] = ring("grp", 5, [P, 4 * W], BF16)
+
+        def turn_half(key, half, engine, source=None):
             if half == 0:
-                staged[key] = ring(sb, "grp", 3, [P, 4 * W], BF16)
-            if key in raw:
-                rows = raw[key][:, 2 * half:2 * half + 2, :]
-            else:
-                rows = raw[key + (half,)][:]
-            words = rows.rearrange("p a k -> p (a k)").bitcast(F32)
+                new_staged(key)
             bank = new_bank("tr")
             for a in range(2):
                 for w in range(2):
-                    nc.tensor.transpose(bank[:, block(2 * a + w)], words[:, 256 * a + w:256 * (a + 1):2], ident[:])
+                    if source is None:
+                        cols = word_columns(raw[key + (half,)], a, w)
+                    elif key[0] == "b":
+                        cols = source[0][:].rearrange("p a c -> p (a c)").bitcast(F32)[:, block(4 * half + 2 * a + w)]
+                    else:
+                        cols = word_columns(source, 2 * half + a, w)
+                    nc.tensor.transpose(bank[:, block(2 * a + w)], cols, ident[:])
             src = bank[:].rearrange("p (a w m) -> p a m w", a=2, w=2)
             out = staged[key][:].bitcast(F32)[:, half * W:(half + 1) * W].rearrange("p (a m w) -> p a m w", a=2, w=2)
             if engine == "s":
@@ -123,84 +144,111 @@ def tile_gmlp_gating_backward_f3_kernel(tc, dy, wo, u, f, n, gamma, beta, ws, et
             else:
                 nc.vector.tensor_copy(out=out, in_=src)
 
-        def turn_input(key):
-            turn_half(key, 0, "s")
-            turn_half(key, 1, "s")
+        def turn(key, source):
+            turn_half(key, 0, "s", source)
+            turn_half(key, 1, "s", source)
 
         def interleave(key, src, engine):
-            staged[key] = ring(sb, "grp", 3, [P, 4 * W], BF16)
+            new_staged(key)
             out = staged[key][:].rearrange("p (c i t) -> p c t i", i=4, t=4)
-            in_ = src[:].rearrange("p t (c i) -> p c t i", i=4)
+            in_ = src.rearrange("p t (c i) -> p c t i", i=4)
             if engine == "s":
                 nc.scalar.copy(out=out, in_=in_)
             elif engine == "v":
                 nc.vector.tensor_copy(out=out, in_=in_)
             else:
-                out = staged[key][:].rearrange("p (c t) -> p c t", t=4)
-                in_ = src[:].rearrange("p t c -> p c t")
-                for j in range(4):
-                    nc.gpsimd.tensor_scalar(out=out[:, block(j), :], in0=in_[:, block(j), :], scalar1=1.0, scalar2=0.0, op0=MULT, op1=mybir.AluOpType.add)
+                width = P // G_PARTS
+                for j in range(G_PARTS):
+                    cs = slice(j * width, (j + 1) * width)
+                    nc.gpsimd.tensor_scalar(out=out[:, cs, :, :], in0=in_[:, cs, :, :], scalar1=1.0, scalar2=0.0, op0=MULT, op1=mybir.AluOpType.add)
 
-        dg_banks = {}
+        df_banks = {}
+        du_banks = {}
+        dfs = {}
         outs = {}
 
         def dg(i):
             h, g = UNITS[i // 4]
             bank = new_bank("dg")
-            dg_banks[i] = bank
-            for t in range(4):
-                mm(bank[:, block(t)], ("dy", h), E4, block(t), ("wo", g), E4, block(i % 4), True, True)
+            df_banks[i] = bank
+            if DIRECT:
+                for t in range(4):
+                    mm(bank[:, block(t)], ("dy", h), E4, block(t), ("wo", g), E4, block(i % 4), True, True)
+            else:
+                mm(bank[:], ("dy", h), E4, block(i % 4), ("wo", g), E4, slice(0, W), True, True)
+            if i < TWICE:
+                bank = new_bank("dg")
+                mm(bank[:], ("dy", h), E4, block(i % 4), ("wo", g), E4, slice(0, W), True, True)
+            du_banks[i] = bank
 
         def df(i):
             un, b = divmod(i, 4)
-            if b == 0:
-                staged[("a", un)] = ring(sb, "dfa", 2, [P, 4 * W], BF16)
-            out = staged[("a", un)][:].rearrange("p (s q t) -> p q t s", s=4, t=4)[:, 32 * b:32 * (b + 1), :, :]
-            nc.vector.tensor_tensor(
-                out=out,
-                in0=dg_banks[i][:].rearrange("p (t q s) -> p q t s", t=4, s=4),
-                in1=raw[("u", un)][:, :, block(b)].rearrange("p t (q s) -> p q t s", s=4),
-                op=MULT,
-            )
+            if DIRECT:
+                if b == 0:
+                    staged[("a", un)] = ring("df", 2, [P, 4 * W], BF16)
+                out = staged[("a", un)][:].rearrange("p (s q t) -> p q t s", s=4, t=4)[:, 32 * b:32 * (b + 1), :, :]
+                nc.vector.tensor_tensor(
+                    out=out,
+                    in0=df_banks[i][:].rearrange("p (t q s) -> p q t s", t=4, s=4),
+                    in1=piece(("u",) + UNITS[un])[:, :, block(b)].rearrange("p t (q s) -> p q t s", s=4),
+                    op=MULT,
+                )
+            else:
+                if b == 0:
+                    dfs[un] = ring("df", 2, [P, 4, W], BF16)
+                nc.vector.tensor_tensor(
+                    out=dfs[un][:, b, :].rearrange("p (w q e) -> p w q e", w=2, e=2),
+                    in0=df_banks[i][:].rearrange("p (q w e) -> p w q e", w=2, e=2),
+                    in1=piece(("u",) + UNITS[un])[:, b, :].rearrange("p (q w e) -> p w q e", w=2, e=2),
+                    op=MULT,
+                )
 
         def du(i):
             un, b = divmod(i, 4)
             if b == 0:
-                outs[("du", un)] = ring(sb, "out", OUT_SLOTS, [P, 4, W], F32)
-            nc.vector.tensor_tensor(
-                out=outs[("du", un)][:, :, block(b)],
-                in0=dg_banks[i][:].rearrange("p (t c) -> p t c", t=4),
-                in1=raw[("f", un)][:, :, block(b)],
-                op=MULT,
-            )
-
-        def store_du(un):
-            h, g = UNITS[un]
-            nc.sync.dma_start(out=rows4(out_0, h, g), in_=outs[("du", un)][:])
-
-        def turn_df(un, halves=range(2)):
-            if halves[0] == 0:
-                staged[("b", un)] = ring(sb, "dfb", 2, [P, 4 * W], BF16)
-            words = staged[("a", un)][:].bitcast(F32)
-            for w in halves:
-                bank = new_bank("tr")
-                for s in range(4):
-                    nc.tensor.transpose(bank[:, block(s)], words[:, 256 * s + w:256 * (s + 1):2], ident[:])
-                nc.scalar.copy(
-                    out=staged[("b", un)][:, w * 2 * W:(w + 1) * 2 * W].rearrange("p (e m s) -> p e m s", e=2, s=4),
-                    in_=bank[:].bitcast(BF16).rearrange("p (s m e) -> p e m s", s=4, e=2),
+                outs[("du", un)] = out_tile()
+            if DIRECT and i >= TWICE:
+                nc.vector.tensor_tensor(
+                    out=outs[("du", un)][:, :, block(b)],
+                    in0=du_banks[i][:].rearrange("p (t c) -> p t c", t=4),
+                    in1=piece(("f",) + UNITS[un])[:, :, block(b)],
+                    op=MULT,
                 )
+            else:
+                nc.vector.tensor_tensor(out=outs[("du", un)][:, b, :], in0=du_banks[i][:], in1=piece(("f",) + UNITS[un])[:, b, :], op=MULT)
+
+        def store_du(un, ts=slice(0, 4)):
+            h, g = UNITS[un]
+            nc.sync.dma_start(out=rows4(out_0, h, g)[:, ts, :], in_=outs[("du", un)][:, ts, :])
+
+        def turn_df(un):
+            if DIRECT:
+                new_staged(("b", un))
+                words = staged[("a", un)][:].bitcast(F32)
+                for w in range(2):
+                    bank = new_bank("tr")
+                    for s in range(4):
+                        nc.tensor.transpose(bank[:, block(s)], words[:, 256 * s + w:256 * (s + 1):2], ident[:])
+                    nc.scalar.copy(
+                        out=staged[("b", un)][:, w * 2 * W:(w + 1) * 2 * W].rearrange("p (e m s) -> p e m s", e=2, s=4),
+                        in_=bank[:].bitcast(BF16).rearrange("p (s m e) -> p e m s", s=4, e=2),
+                    )
+            else:
+                turn(("b", un), (dfs[un], 0))
+
+        def il_a(un):
+            if not DIRECT:
+                interleave(("a", un), dfs[un][:], A_ENGINES[un])
 
         vs = {}
 
         def make_v(g, jh, word_halves=range(2)):
             if word_halves[0] == 0:
-                vs[(g, jh)] = ring(sb, "vs", 2, [P, 4, W], BF16)
-            words = raw[("n", g, jh)][:].rearrange("p a c -> p (a c)").bitcast(F32)
+                vs[(g, jh)] = ring("vs", 2, [P, 4, W], BF16)
             for w in word_halves:
                 bank = new_bank("tr")
                 for a in range(4):
-                    nc.tensor.transpose(bank[:, block(a)], words[:, 256 * a + w:256 * (a + 1):2], ident[:])
+                    nc.tensor.transpose(bank[:, block(a)], word_columns(raw[("n", jh, g)], a, w), ident[:])
                 halves = bank[:].bitcast(BF16).rearrange("p (a m e) -> p e m a", a=4, e=2)
                 for e in range(2):
                     s = 2 * w + e
@@ -231,17 +279,25 @@ def tile_gmlp_gating_backward_f3_kernel(tc, dy, wo, u, f, n, gamma, beta, ws, et
 
         def dn(g, jt):
             if jt % 4 == 0:
-                outs[("dn", g, jt // 4)] = ring(sb, "out", OUT_SLOTS, [P, 4, W], F32)
-            nc.vector.tensor_tensor(
-                out=outs[("dn", g, jt // 4)][:, jt % 4, :].rearrange("p (q s) -> p q s", s=4),
-                in0=acc[("dv", g, jt)][:].rearrange("p (s q) -> p q s", s=4),
-                in1=gam_rows[:, g * W:(g + 1) * W].rearrange("p (q s) -> p q s", s=4),
-                op=MULT,
-            )
-
-        def store_dn(g, jh, bs=slice(0, 4)):
-            dst = out_1[jh * W:(jh + 1) * W, g * W:(g + 1) * W].rearrange("(b p) c -> p b c", b=4)
-            nc.sync.dma_start(out=dst[:, bs, :], in_=outs[("dn", g, jh)][:, bs, :])
+                outs[("dn", g, jt // 4)] = out_tile()
+            if DIRECT:
+                nc.vector.tensor_tensor(
+                    out=outs[("dn", g, jt // 4)][:, jt % 4, :].rearrange("p (q s) -> p q s", s=4),
+                    in0=acc[("dv", g, jt)][:].rearrange("p (s q) -> p q s", s=4),
+                    in1=gam_rows[:, g * W:(g + 1) * W].rearrange("p (q s) -> p q s", s=4),
+                    op=MULT,
+                )
+            else:
+                nc.vector.tensor_tensor(
+                    out=outs[("dn", g, jt // 4)][:, jt % 4, :].rearrange("p (q w e) -> p q w e", w=2, e=2),
+                    in0=acc[("dv", g, jt)][:].rearrange("p (w q e) -> p q w e", w=2, e=2),
+                    in1=gam_rows[:, g * W:(g + 1) * W].rearrange("p (q w e) -> p q w e", w=2, e=2),
+                    op=MULT,
+                )
+            if jt % 2 == 1:
+                dst = out_1[jt // 4 * W:(jt // 4 + 1) * W, g * W:(g + 1) * W].rearrange("(b p) c -> p b c", b=4)
+                bs = slice(jt % 4 - 1, jt % 4 + 1)
+                nc.sync.dma_start(out=dst[:, bs, :], in_=outs[("dn", g, jt // 4)][:, bs, :])
 
         def dws(h, k, groups=range(3), role_name="acc"):
             jh, t = divmod(k, 4)
@@ -254,16 +310,16 @@ def tile_gmlp_gating_backward_f3_kernel(tc, dy, wo, u, f, n, gamma, beta, ws, et
         def step(h, k):
             jh, t = divmod(k, 4)
             if t == 0:
-                outs[("step", h, jh)] = ring(sb, "out", OUT_SLOTS, [P, 4, W], F32)
+                outs[("step", h, jh)] = out_tile()
             nc.scalar.activation(
                 out=outs[("step", h, jh)][:, t, :],
                 in_=acc[("dws", h, k)][:],
                 func=ACT.Copy,
                 scale=eta32[:, 4 * h + t:4 * h + t + 1],
             )
-
-        def store_step(h, jh, ts):
-            nc.sync.dma_start(out=rows4(out_2, h, jh)[:, ts, :], in_=outs[("step", h, jh)][:, ts, :])
+            if t % 2 == 1:
+                ts = slice(t - 1, t + 1)
+                nc.sync.dma_start(out=rows4(out_2, h, jh)[:, ts, :], in_=outs[("step", h, jh)][:, ts, :])
 
         gam16 = sb.tile([P, 3, 4], BF16, name="gam16")
         bet16 = sb.tile([P, 3, 4], BF16, name="bet16")
@@ -273,48 +329,40 @@ def tile_gmlp_gating_backward_f3_kernel(tc, dy, wo, u, f, n, gamma, beta, ws, et
         eta32 = sb.tile([P, 8], F32, name="eta32")
         gam_rows = sb.tile([P, F], BF16, name="gam_rows")
 
-        def load_half(key, half, src):
-            raw[key + (half,)] = ring(sb, "first", 4, [P, 2, W], BF16)
-            nc.sync.dma_start(out=raw[key + (half,)][:], in_=src[:, 2 * half:2 * half + 2, :])
-
-        dy_first = rows4(dy, 0, 0)
-        wo_first = wo[0:W, :].rearrange("(b m) k -> m b k", b=4)
-        load_half(("dy", 0), 0, dy_first)
-        load_half(("wo", 0), 0, wo_first)
-        load_half(("dy", 0), 1, dy_first)
+        load_half(("dy", 0), 0, rows4(dy, 0, 0))
+        load_half(("wo", 0), 0, wo_rows(0))
+        load_half(("dy", 0), 1, rows4(dy, 0, 0))
         nc.scalar.dma_start(out=gam16[:], in_=gamma.rearrange("(g q s) -> q g s", g=3, s=4))
         nc.scalar.dma_start(out=bet16[:], in_=beta.rearrange("(g q s) -> q g s", g=3, s=4))
-        load(("u", 0), rows4(u, 0, 0))
-        load_half(("wo", 0), 1, wo_first)
-        load(("f", 0), rows4(f, 0, 0))
-        load_n(0, 0)
+        load_half(("wo", 0), 1, wo_rows(0))
+        load("u", u, 0, 0, 1)
+        load("f", f, 0, 0, 1)
+        load("n", n, 0, 0, 1)
         load_wo(1)
-        load_unit(1)
-        load_n(1, 0)
+        load("u", u, 0, 1, 2)
+        load("f", f, 0, 1, 2)
         load_wo(2)
         nc.sync.dma_start(out=eta16[:], in_=eta.rearrange("(h p t) -> p h t", h=2, t=4))
-        load_n(2, 0)
-        load_unit(2)
-        load_dy(1)
-        load_unit(3)
-        load_ws(0, 0)
-        load_ws(1, 0)
-        load_ws(0, 1)
-        load_ws(1, 1)
+        load("n", n, 0, 1, 2)
+        load("dy", dy, 1, 0, 1)
+        load("u", u, 1, 0, 1)
+        load("f", f, 1, 0, 1)
+        load("ws", ws, 0, 0, 2)
+        load("ws", ws, 1, 0, 2)
+        load("u", u, 1, 1, 2)
+        load("f", f, 1, 1, 2)
+        load("n", n, 1, 0, 3)
 
         nc.scalar.activation(out=gam[:], in_=gam16[:].rearrange("p g s -> p (g s)"), func=ACT.Identity)
         turn_half(("dy", 0), 0, "s")
         turn_half(("wo", 0), 0, "v")
-        turn_half(("dy", 0), 1, "s")
         quantize(("dy", 0), E4, "dyq", 2, 0, 2)
         quantize(("wo", 0), E4, "woq", 3, 0, 2)
-        quantize(("dy", 0), E4, "dyq", 2, 1, 2)
         turn_half(("wo", 0), 1, "s")
+        turn_half(("dy", 0), 1, "v")
+        quantize(("wo", 0), E4, "woq", 3, 1, 2)
+        quantize(("dy", 0), E4, "dyq", 2, 1, 2)
         nc.scalar.activation(out=bet[:], in_=bet16[:].rearrange("p g s -> p (g s)"), func=ACT.Identity)
-        dg(0)
-        dg(1)
-        for g in range(3):
-            spread_gamma(g)
 
         def q_dy(h):
             quantize(("dy", h), E4, "dyq", 2)
@@ -335,19 +383,13 @@ def tile_gmlp_gating_backward_f3_kernel(tc, dy, wo, u, f, n, gamma, beta, ws, et
             quantize(("b", un), E5, "bq", 5)
 
         def il_ws(h, jh):
-            interleave(("ws", h, jh), raw[("ws", h, jh)], WS_ENGINE)
+            interleave(("ws", h, jh), piece(("ws", h, jh)), WS_ENGINES[2 * jh + h])
 
         def il_v(g, jh):
-            interleave(("v", g, jh), vs[(g, jh)], V_ENGINES[3 * jh + g])
+            interleave(("v", g, jh), vs[(g, jh)][:], V_ENGINES[3 * jh + g])
 
         def eta_f32():
             nc.scalar.activation(out=eta32[:], in_=eta16[:].rearrange("p h t -> p (h t)"), func=ACT.Identity)
-
-        def late_loads():
-            load_unit(4)
-            for g in range(3):
-                load_n(g, 1)
-            load_unit(5)
 
         def narrow_tr():
             role["tr"] = (3, 4)
@@ -361,117 +403,86 @@ def tile_gmlp_gating_backward_f3_kernel(tc, dy, wo, u, f, n, gamma, beta, ws, et
             for fn, args in plan[(i, where)]:
                 fn(*args)
 
-        dg_step = {j: j - 2 if j >= 2 else -1 for j in range(24)}
-        dg_step[2] = 1
-        dg_step[4] = 3
-        first, second = range(0, 1), range(1, 2)
-        at(0, 3, quantize, ("wo", 0), E4, "woq", 3, 1, 2)
-        at(1, 1, make_v, 0, 0, first)
-        at(1, 1, turn_input, ("wo", 1))
-        at(1, 1, make_v, 0, 0, second)
+        at(1, 3, turn, ("wo", 1), raw[("wo", 1)])
         at(2, 3, q_wo, 1)
+        for g in range(3):
+            at(2, 3, spread_gamma, g)
+        at(2, 3, make_v, 0, 0)
         for un in range(5):
-            at(4 * un + 4, 2, q_a, un)
-        at(4, 1, turn_df, 0)
-        at(4, 1, turn_input, ("wo", 2))
-        at(4, 3, il_v, 0, 0)
-        at(5, 0, make_v, 1, 0)
-        at(5, 3, q_v, 0, 0)
-        at(5, 3, q_wo, 2)
-        at(6, 3, q_b, 0)
-        at(7, 0, make_v, 2, 0)
-        at(7, 3, il_v, 1, 0)
-        at(7, 3, late_loads)
-        at(7, 3, store_du, 0)
-        at(7, 3, store_du, 1)
-        for un in range(2, 5):
+            at(4 * un + 4, 2, turn_df, un)
+            at(4 * un + 4, 2, il_a, un)
+            at(4 * un + 5, 3, q_a, un)
+            at(4 * un + 6, 3, q_b, un)
             at(4 * un + 3, 3, store_du, un)
-        at(8, 1, turn_input, ("dy", 1))
-        at(8, 1, turn_df, 1)
-        at(8, 3, q_v, 1, 0)
-        at(9, 1, eta_f32)
-        at(9, 1, il_v, 2, 0)
-        at(9, 3, q_dy, 1)
-        at(11, 3, q_b, 1)
-        at(12, 1, turn_df, 2)
+        at(5, 0, turn, ("wo", 2), raw[("wo", 2)])
+        at(5, 0, il_v, 0, 0)
+        at(6, 3, q_wo, 2)
+        at(6, 3, make_v, 1, 0)
+        at(7, 3, q_v, 0, 0)
+        at(7, 3, il_v, 1, 0)
+        at(8, 3, make_v, 2, 0)
+        at(9, 0, turn, ("dy", 1), raw[("dy", 1, 0)])
+        at(9, 3, q_v, 1, 0)
+        at(9, 3, eta_f32)
+        at(10, 3, q_dy, 1)
+        at(10, 3, il_v, 2, 0)
         at(12, 3, q_v, 2, 0)
         at(12, 3, narrow_tr)
         at(12, 3, il_ws, 0, 0)
-        at(14, 3, q_b, 2)
+        at(13, 3, il_ws, 1, 0)
         for k in range(4):
             at(15, 1, dws, 0, k)
             at(15, 1, step, 0, k)
-        at(15, 3, store_step, 0, 0, slice(0, 4))
-        at(15, 0, il_ws, 1, 0)
-        at(15, 3, q_ws, 0, 0)
-        at(16, 3, q_ws, 1, 0)
-        at(16, 1, turn_df, 3)
-        at(16, 1, il_ws, 0, 1)
-        at(17, 0, il_ws, 1, 1)
-        at(18, 0, make_v, 0, 1)
-        at(18, 3, q_ws, 0, 1)
-        at(18, 3, q_b, 3)
-        at(19, 0, make_v, 1, 1)
-        at(19, 1, q_ws, 1, 1)
-        at(20, 1, il_v, 0, 1)
-        at(20, 1, turn_df, 4)
-        at(20, 3, il_v, 1, 1)
-        at(21, 0, make_v, 2, 1)
-        at(21, 0, il_v, 2, 1)
-        at(21, 3, q_v, 0, 1)
+        at(14, 3, q_ws, 0, 0)
+        at(15, 3, q_ws, 1, 0)
+        at(15, 3, il_ws, 0, 1)
+        at(16, 3, il_ws, 1, 1)
+        at(17, 3, q_ws, 0, 1)
+        at(17, 3, make_v, 0, 1)
+        at(18, 3, q_ws, 1, 1)
+        at(18, 3, il_v, 0, 1)
+        at(18, 3, make_v, 1, 1)
+        at(19, 3, il_v, 1, 1)
+        at(19, 3, make_v, 2, 1)
+        at(20, 3, q_v, 0, 1)
+        at(20, 3, il_v, 2, 1)
         at(21, 3, q_v, 1, 1)
-        at(22, 1, q_b, 4)
-        at(22, 1, q_v, 2, 1)
-        jobs = [(dv, dn, 0, jt) for jt in range(8)] + [(dv, dn, 1, jt) for jt in range(8)] + [(dws, step, 0, k) for k in range(4, 8)]
-        slots = [(17, 2), (17, 3), (18, 1), (18, 2), (19, 2), (19, 3), (20, 3), (20, 3), (21, 1), (21, 1), (21, 2), (21, 3), (22, 1), (22, 2), (22, 3), (22, 3), (23, 1), (23, 1), (23, 1), (23, 1)]
-        make_slots = [(17, 1), (17, 1)] + slots[:-2]
-        make_slots[4:6] = [(19, 1), (19, 1)]
-        for k, (make, read, x, y) in enumerate(jobs):
-            at(*make_slots[k], make, x, y)
-            if k >= 2:
-                make, read, x, y = jobs[k - 2]
-                at(*slots[k - 2], read, x, y)
-                if y % 4 == 3:
-                    at(*slots[k - 2], store_dn if read is dn else store_step, x, y // 4, slice(0, 4))
-        at(23, 1, step, 0, 6)
-        at(23, 1, step, 0, 7)
-        at(23, 1, store_step, 0, 1, slice(0, 4))
+        at(21, 3, q_v, 2, 1)
+        for jt in range(8):
+            at(17 + jt // 3, 3, dv, 0, jt)
+            at(17 + jt // 3, 3, dn, 0, jt)
+        for jt in range(8):
+            at(21, 3, dv, 1, jt)
+            at(21, 3, dn, 1, jt)
+        for k in range(4, 8):
+            at(21, 3, dws, 0, k)
+            at(21, 3, step, 0, k)
 
         for i in range(24):
             run(i, 0)
-            for j in range(24):
-                if dg_step[j] == i:
-                    dg(j)
+            dg(i)
             run(i, 1)
             df(i)
             run(i, 2)
-            if i < 21:
+            if i < 23:
                 du(i)
             run(i, 3)
 
+        turn_df(5)
+        il_a(5)
+        du(23)
+        store_du(5)
+        q_a(5)
+        q_b(5)
         for k in range(3):
             dws(1, k, range(2))
-        turn_df(5)
-        q_a(5)
         role["tail"] = (0, 1, 2, 3, 4)
-        for jt in range(3):
-            du(21 + jt)
-            dv(2, jt, "tail")
-        store_du(5)
-        q_b(5)
-        dv(2, 3, "tail")
-        dv(2, 4, "tail")
         for jt in range(8):
+            dv(2, jt, "tail")
             dn(2, jt)
-            if jt < 3:
-                dv(2, 5 + jt, "tail")
-                dws(1, jt, range(2, 3))
-                step(1, jt)
-            if jt % 2 == 1:
-                store_dn(2, jt // 4, slice(jt % 4 - 1, jt % 4 + 1))
-        store_step(1, 0, slice(0, 2))
+            if jt in (1, 3, 5):
+                dws(1, jt // 2, range(2, 3))
+                step(1, jt // 2)
         for k in range(3, 8):
             dws(1, k)
             step(1, k)
-            if k % 2 == 1:
-                store_step(1, k // 4, slice(k % 4 - 1, k % 4 + 1))

@@ -17,13 +17,9 @@ MULT = mybir.AluOpType.mult
 
 P = 128
 W = 512
-UNITS = [(h, g) for h in range(2) for g in range(3)]
-DIRECT = False
-TWICE = 0
-WS_ENGINES = "ssss"
-V_ENGINES = "ssssss"
-A_ENGINES = "vvvvvv"
-G_PARTS = 4
+UNITS = [(0, 0), (1, 0), (0, 1), (0, 2), (1, 1), (1, 2)]
+OWN_PASS = (0, 1)
+LATE_DU = 20
 
 
 def tile_gmlp_gating_backward_f3_kernel(tc, dy, wo, u, f, n, gamma, beta, ws, eta, out_0, out_1, out_2):
@@ -33,28 +29,30 @@ def tile_gmlp_gating_backward_f3_kernel(tc, dy, wo, u, f, n, gamma, beta, ws, et
         ps = ctx.enter_context(tc.psum_pool(name="ps", bufs=1))
         turns = {}
 
+        def rotate(pool, tags, shape, dtype, **kw):
+            k = turns.get(tags, 0)
+            turns[tags] = k + 1
+            tag = tags[k % len(tags)]
+            return pool.tile(shape, dtype, name=tag, tag=tag, **kw)
+
         def slot(tag, shape, dtype):
             return sb.tile(shape, dtype, name=tag, tag=tag, align_bytes=64)
 
         def ring(name, slots, shape, dtype):
-            k = turns.get(name, 0)
-            turns[name] = k + 1
-            return slot("%s%d" % (name, k % slots), shape, dtype)
+            return rotate(sb, tuple("%s%d" % (name, k) for k in range(slots)), shape, dtype, align_bytes=64)
+
+        out_tags = ("out0", "out1", "out2", "out3", "u_one0", "f_one0", "dy_one1", "u_one1", "f_one1", "wo1", "ws_wide0", "ws_wide1", "n_one0")
 
         def out_tile():
-            tags = ["out0", "out1", "out2", "u_wide0", "f_wide0", "n_wide0"]
-            k = turns.get("out", 0)
-            turns["out"] = k + 1
-            return slot(tags[k % len(tags)], [P, 4, W], F32)
+            return rotate(sb, out_tags, [P, 2, W], F32, align_bytes=64)
+
+        role = {}
+
+        def set_banks(name, banks):
+            role[name] = tuple("bank%d" % b for b in banks)
 
         def new_bank(name):
-            tags = role[name]
-            k = turns.get(tags, 0)
-            turns[tags] = k + 1
-            tag = "bank%d" % tags[k % len(tags)]
-            return ps.tile([P, W], F32, name=tag, tag=tag)
-
-        role = {"dg": (0, 1, 2), "tr": (3, 4, 5, 6, 7), "acc": (5, 6, 7)}
+            return rotate(ps, role[name], [P, W], F32)
 
         ident = sb.tile([P, P], F32, name="ident")
         make_identity(nc, ident[:])
@@ -74,10 +72,9 @@ def tile_gmlp_gating_backward_f3_kernel(tc, dy, wo, u, f, n, gamma, beta, ws, et
             tile, j = raw[key]
             return tile[:, :, j * W:(j + 1) * W]
 
-        def word_columns(source, a, w):
-            tile, j = source
-            width = tile.shape[2] // 2
-            base = a * width + j * 256
+        def word_columns(key, a, w):
+            tile, j = raw[key]
+            base = a * tile.shape[2] // 2 + j * 256
             return tile[:].rearrange("p a c -> p (a c)").bitcast(F32)[:, base + w:base + 256:2]
 
         def wo_rows(g):
@@ -95,10 +92,13 @@ def tile_gmlp_gating_backward_f3_kernel(tc, dy, wo, u, f, n, gamma, beta, ws, et
 
         codes = {}
         staged = {}
+        banks = {}
+        formats = {"dy": (E4, 2), "wo": (E4, 3), "ws": (E4, 4), "v": (E4, 6), "a": (E5, 4), "b": (E5, 5)}
 
-        def quantize(key, fmt, name, slots, part=0, parts=1):
+        def quantize(key, part=0, parts=1):
+            fmt, slots = formats[key[0]]
             if part == 0:
-                codes[key] = (ring(name + "c", slots, [P, W], U32), ring(name + "s", slots, [P, W], U8))
+                codes[key] = (ring(key[0] + "_codes", slots, [P, W], U32), ring(key[0] + "_scales", slots, [P, W], U8))
             width = W // parts
             cols = slice(part * width, (part + 1) * width)
             nc.vector.quantize_mx(
@@ -107,13 +107,13 @@ def tile_gmlp_gating_backward_f3_kernel(tc, dy, wo, u, f, n, gamma, beta, ws, et
                 in_=staged[key][:, 4 * part * width:4 * (part + 1) * width],
             )
 
-        def mm(bank, lhs_key, lhs_fmt, lhs_cols, rhs_key, rhs_fmt, rhs_cols, start, stop):
+        def mm(bank, lhs, lhs_cols, rhs, rhs_cols, start, stop):
             nc.tensor.matmul_mx(
                 out=bank,
-                lhsT=codes[lhs_key][0][:, lhs_cols].bitcast(lhs_fmt),
-                lhsT_scale=codes[lhs_key][1][:, lhs_cols],
-                rhs=codes[rhs_key][0][:, rhs_cols].bitcast(rhs_fmt),
-                rhs_scale=codes[rhs_key][1][:, rhs_cols],
+                lhsT=codes[lhs][0][:, lhs_cols].bitcast(formats[lhs[0]][0]),
+                lhsT_scale=codes[lhs][1][:, lhs_cols],
+                rhs=codes[rhs][0][:, rhs_cols].bitcast(formats[rhs[0]][0]),
+                rhs_scale=codes[rhs][1][:, rhs_cols],
                 start=start,
                 stop=stop,
             )
@@ -122,204 +122,168 @@ def tile_gmlp_gating_backward_f3_kernel(tc, dy, wo, u, f, n, gamma, beta, ws, et
             return slice(j * P, (j + 1) * P)
 
         def new_staged(key):
-            staged[key] = ring("grp", 5, [P, 4 * W], BF16)
+            staged[key] = ring("staged", 7, [P, 4 * W], BF16)
 
-        def turn_half(key, half, engine, source=None):
-            if half == 0:
-                new_staged(key)
-            bank = new_bank("tr")
+        def copy_on(engine, out, in_):
+            if engine is nc.scalar:
+                nc.scalar.copy(out=out, in_=in_)
+            else:
+                nc.vector.tensor_copy(out=out, in_=in_)
+
+        def turn_rows(key, half):
+            bank = new_bank("turn")
+            banks[key + (half,)] = bank
             for a in range(2):
                 for w in range(2):
-                    if source is None:
-                        cols = word_columns(raw[key + (half,)], a, w)
-                    elif key[0] == "b":
-                        cols = source[0][:].rearrange("p a c -> p (a c)").bitcast(F32)[:, block(4 * half + 2 * a + w)]
+                    if key in raw:
+                        cols = word_columns(key, 2 * half + a, w)
                     else:
-                        cols = word_columns(source, 2 * half + a, w)
+                        cols = word_columns(key + (half,), a, w)
                     nc.tensor.transpose(bank[:, block(2 * a + w)], cols, ident[:])
-            src = bank[:].rearrange("p (a w m) -> p a m w", a=2, w=2)
-            out = staged[key][:].bitcast(F32)[:, half * W:(half + 1) * W].rearrange("p (a m w) -> p a m w", a=2, w=2)
-            if engine == "s":
-                nc.scalar.copy(out=out, in_=src)
-            else:
-                nc.vector.tensor_copy(out=out, in_=src)
 
-        def turn(key, source):
-            turn_half(key, 0, "s", source)
-            turn_half(key, 1, "s", source)
+        def stage_rows(key, half, engine=nc.scalar):
+            if half == 0:
+                new_staged(key)
+            out = staged[key][:].bitcast(F32)[:, half * W:(half + 1) * W].rearrange("p (a m w) -> p a m w", a=2, w=2)
+            copy_on(engine, out, banks[key + (half,)][:].rearrange("p (a w m) -> p a m w", a=2, w=2))
 
         def interleave(key, src, engine):
             new_staged(key)
-            out = staged[key][:].rearrange("p (c i t) -> p c t i", i=4, t=4)
-            in_ = src.rearrange("p t (c i) -> p c t i", i=4)
-            if engine == "s":
-                nc.scalar.copy(out=out, in_=in_)
-            elif engine == "v":
-                nc.vector.tensor_copy(out=out, in_=in_)
-            else:
-                width = P // G_PARTS
-                for j in range(G_PARTS):
-                    cs = slice(j * width, (j + 1) * width)
-                    nc.gpsimd.tensor_scalar(out=out[:, cs, :, :], in0=in_[:, cs, :, :], scalar1=1.0, scalar2=0.0, op0=MULT, op1=mybir.AluOpType.add)
+            copy_on(engine, staged[key][:].rearrange("p (c i t) -> p c t i", i=4, t=4), src.rearrange("p t (c i) -> p c t i", i=4))
 
-        df_banks = {}
-        du_banks = {}
-        dfs = {}
         outs = {}
 
         def dg(i):
             h, g = UNITS[i // 4]
             bank = new_bank("dg")
-            df_banks[i] = bank
-            if DIRECT:
-                for t in range(4):
-                    mm(bank[:, block(t)], ("dy", h), E4, block(t), ("wo", g), E4, block(i % 4), True, True)
-            else:
-                mm(bank[:], ("dy", h), E4, block(i % 4), ("wo", g), E4, slice(0, W), True, True)
-            if i < TWICE:
-                bank = new_bank("dg")
-                mm(bank[:], ("dy", h), E4, block(i % 4), ("wo", g), E4, slice(0, W), True, True)
-            du_banks[i] = bank
+            banks[("df", i)] = bank
+            for t in range(4):
+                mm(bank[:, block(t)], ("dy", h), block(t), ("wo", g), block(i % 4), True, True)
+
+        def dg_rows(i, name="dg"):
+            h, g = UNITS[i // 4]
+            bank = new_bank(name)
+            banks[("du", i)] = bank
+            mm(bank[:], ("dy", h), block(i % 4), ("wo", g), slice(0, W), True, True)
 
         def df(i):
             un, b = divmod(i, 4)
-            if DIRECT:
-                if b == 0:
-                    staged[("a", un)] = ring("df", 2, [P, 4 * W], BF16)
-                out = staged[("a", un)][:].rearrange("p (s q t) -> p q t s", s=4, t=4)[:, 32 * b:32 * (b + 1), :, :]
-                nc.vector.tensor_tensor(
-                    out=out,
-                    in0=df_banks[i][:].rearrange("p (t q s) -> p q t s", t=4, s=4),
-                    in1=piece(("u",) + UNITS[un])[:, :, block(b)].rearrange("p t (q s) -> p q t s", s=4),
-                    op=MULT,
-                )
-            else:
-                if b == 0:
-                    dfs[un] = ring("df", 2, [P, 4, W], BF16)
-                nc.vector.tensor_tensor(
-                    out=dfs[un][:, b, :].rearrange("p (w q e) -> p w q e", w=2, e=2),
-                    in0=df_banks[i][:].rearrange("p (q w e) -> p w q e", w=2, e=2),
-                    in1=piece(("u",) + UNITS[un])[:, b, :].rearrange("p (q w e) -> p w q e", w=2, e=2),
-                    op=MULT,
-                )
+            if b == 0:
+                staged[("a", un)] = ring("df", 3, [P, 4 * W], BF16)
+            nc.vector.tensor_tensor(
+                out=staged[("a", un)][:].rearrange("p (s q t) -> p q t s", s=4, t=4)[:, 32 * b:32 * (b + 1), :, :],
+                in0=banks[("df", i)][:].rearrange("p (t q s) -> p q t s", t=4, s=4),
+                in1=piece(("u",) + UNITS[un])[:, :, block(b)].rearrange("p t (q s) -> p q t s", s=4),
+                op=MULT,
+            )
 
         def du(i):
             un, b = divmod(i, 4)
-            if b == 0:
-                outs[("du", un)] = out_tile()
-            if DIRECT and i >= TWICE:
+            h, g = UNITS[un]
+            if un in OWN_PASS:
+                if b % 2 == 0:
+                    outs[("du", i // 2)] = out_tile()
+                tile = outs[("du", i // 2)]
+                nc.vector.tensor_tensor(out=tile[:, b % 2, :], in0=banks[("du", i)][:], in1=piece(("f", h, g))[:, b, :], op=MULT)
+                if b % 2 == 1:
+                    nc.sync.dma_start(out=rows4(out_0, h, g)[:, b - 1:b + 1, :], in_=tile[:])
+            else:
+                if b % 2 == 0:
+                    outs[("du", i // 2)] = out_tile()
+                tile = outs[("du", i // 2)][:].rearrange("p a c -> p (a c)").rearrange("p (t c) -> p t c", t=4)
                 nc.vector.tensor_tensor(
-                    out=outs[("du", un)][:, :, block(b)],
-                    in0=du_banks[i][:].rearrange("p (t c) -> p t c", t=4),
-                    in1=piece(("f",) + UNITS[un])[:, :, block(b)],
+                    out=tile[:, :, block(b % 2)],
+                    in0=banks[("df", i)][:].rearrange("p (t c) -> p t c", t=4),
+                    in1=piece(("f", h, g))[:, :, block(b)],
                     op=MULT,
                 )
-            else:
-                nc.vector.tensor_tensor(out=outs[("du", un)][:, b, :], in0=du_banks[i][:], in1=piece(("f",) + UNITS[un])[:, b, :], op=MULT)
+                if b % 2 == 1:
+                    nc.sync.dma_start(out=rows4(out_0, h, g)[:, :, (b - 1) * P:(b + 1) * P], in_=tile)
 
-        def store_du(un, ts=slice(0, 4)):
-            h, g = UNITS[un]
-            nc.sync.dma_start(out=rows4(out_0, h, g)[:, ts, :], in_=outs[("du", un)][:, ts, :])
+        def turn_df(un, w):
+            bank = new_bank("turn")
+            banks[("b", un, w)] = bank
+            words = staged[("a", un)][:].bitcast(F32)
+            for s in range(4):
+                nc.tensor.transpose(bank[:, block(s)], words[:, 256 * s + w:256 * (s + 1):2], ident[:])
 
-        def turn_df(un):
-            if DIRECT:
+        def stage_df(un, w, engine=nc.scalar):
+            if w == 0:
                 new_staged(("b", un))
-                words = staged[("a", un)][:].bitcast(F32)
-                for w in range(2):
-                    bank = new_bank("tr")
-                    for s in range(4):
-                        nc.tensor.transpose(bank[:, block(s)], words[:, 256 * s + w:256 * (s + 1):2], ident[:])
-                    nc.scalar.copy(
-                        out=staged[("b", un)][:, w * 2 * W:(w + 1) * 2 * W].rearrange("p (e m s) -> p e m s", e=2, s=4),
-                        in_=bank[:].bitcast(BF16).rearrange("p (s m e) -> p e m s", s=4, e=2),
-                    )
-            else:
-                turn(("b", un), (dfs[un], 0))
-
-        def il_a(un):
-            if not DIRECT:
-                interleave(("a", un), dfs[un][:], A_ENGINES[un])
+            copy_on(
+                engine,
+                staged[("b", un)][:, w * 2 * W:(w + 1) * 2 * W].rearrange("p (e m s) -> p e m s", e=2, s=4),
+                banks[("b", un, w)][:].bitcast(BF16).rearrange("p (s m e) -> p e m s", s=4, e=2),
+            )
 
         vs = {}
 
-        def make_v(g, jh, word_halves=range(2)):
-            if word_halves[0] == 0:
-                vs[(g, jh)] = ring("vs", 2, [P, 4, W], BF16)
-            for w in word_halves:
-                bank = new_bank("tr")
-                for a in range(4):
-                    nc.tensor.transpose(bank[:, block(a)], word_columns(raw[("n", jh, g)], a, w), ident[:])
-                halves = bank[:].bitcast(BF16).rearrange("p (a m e) -> p e m a", a=4, e=2)
-                for e in range(2):
-                    s = 2 * w + e
-                    nc.scalar.activation(
-                        out=vs[(g, jh)][:, s, :].rearrange("p (m a) -> p m a", a=4),
-                        in_=halves[:, e, :, :],
-                        func=ACT.Identity,
-                        scale=gam[:, 4 * g + s:4 * g + s + 1],
-                        bias=bet[:, 4 * g + s:4 * g + s + 1],
-                    )
+        def turn_n(g, jh, w):
+            bank = new_bank("turn")
+            banks[("n", g, jh, w)] = bank
+            for a in range(4):
+                nc.tensor.transpose(bank[:, block(a)], word_columns(("n", jh, g), a, w), ident[:])
 
-        def spread_gamma(g):
-            bank = new_bank("tr")
-            for s in range(4):
-                nc.tensor.transpose(bank[:, block(s)], gam[:, 4 * g + s:4 * g + s + 1].to_broadcast([P, P]), ident[:])
-            nc.scalar.copy(
-                out=gam_rows[:, g * W:(g + 1) * W].rearrange("p (q s) -> p q s", s=4),
-                in_=bank[:].rearrange("p (s q) -> p q s", s=4),
-            )
+        def make_v(g, jh, w):
+            if w == 0:
+                vs[(g, jh)] = ring("v_rows", 2, [P, 4, W], BF16)
+            halves = banks[("n", g, jh, w)][:].bitcast(BF16).rearrange("p (a m e) -> p e m a", a=4, e=2)
+            for e in range(2):
+                s = 2 * w + e
+                nc.scalar.activation(
+                    out=vs[(g, jh)][:, s, :].rearrange("p (m a) -> p m a", a=4),
+                    in_=halves[:, e, :, :],
+                    func=ACT.Identity,
+                    scale=gam[:, 4 * g + s:4 * g + s + 1],
+                    bias=bet[:, 4 * g + s:4 * g + s + 1],
+                )
 
-        acc = {}
+        gam_rows = {}
 
-        def dv(g, jt, role_name="acc"):
-            bank = new_bank(role_name)
-            acc[("dv", g, jt)] = bank
-            for h in range(2):
-                mm(bank[:], ("ws", h, jt // 4), E4, block(jt % 4), ("a", UNITS.index((h, g))), E5, slice(0, W), h == 0, h == 1)
+        def load_gamma_rows(g):
+            gam_rows[g] = slot("gamma_rows%d" % g, [P, W], BF16)
+            nc.sync.dma_start(out=gam_rows[g][:], in_=gamma[g * W:(g + 1) * W].partition_broadcast(P))
+
+        def dv(g, jt, halves=range(2), name="acc"):
+            if halves[0] == 0:
+                banks[("dv", g, jt)] = new_bank(name)
+            for h in halves:
+                mm(banks[("dv", g, jt)][:], ("ws", h, jt // 4), block(jt % 4), ("a", UNITS.index((h, g))), slice(0, W), h == 0, h == 1)
 
         def dn(g, jt):
-            if jt % 4 == 0:
-                outs[("dn", g, jt // 4)] = out_tile()
-            if DIRECT:
-                nc.vector.tensor_tensor(
-                    out=outs[("dn", g, jt // 4)][:, jt % 4, :].rearrange("p (q s) -> p q s", s=4),
-                    in0=acc[("dv", g, jt)][:].rearrange("p (s q) -> p q s", s=4),
-                    in1=gam_rows[:, g * W:(g + 1) * W].rearrange("p (q s) -> p q s", s=4),
-                    op=MULT,
-                )
-            else:
-                nc.vector.tensor_tensor(
-                    out=outs[("dn", g, jt // 4)][:, jt % 4, :].rearrange("p (q w e) -> p q w e", w=2, e=2),
-                    in0=acc[("dv", g, jt)][:].rearrange("p (w q e) -> p q w e", w=2, e=2),
-                    in1=gam_rows[:, g * W:(g + 1) * W].rearrange("p (q w e) -> p q w e", w=2, e=2),
-                    op=MULT,
-                )
+            if jt % 2 == 0:
+                outs[("dn", g, jt // 2)] = out_tile()
+            tile = outs[("dn", g, jt // 2)]
+            nc.vector.tensor_tensor(
+                out=tile[:, jt % 2, :].rearrange("p (q s) -> p q s", s=4),
+                in0=banks[("dv", g, jt)][:].rearrange("p (s q) -> p q s", s=4),
+                in1=gam_rows[g][:].rearrange("p (q s) -> p q s", s=4),
+                op=MULT,
+            )
             if jt % 2 == 1:
-                dst = out_1[jt // 4 * W:(jt // 4 + 1) * W, g * W:(g + 1) * W].rearrange("(b p) c -> p b c", b=4)
-                bs = slice(jt % 4 - 1, jt % 4 + 1)
-                nc.sync.dma_start(out=dst[:, bs, :], in_=outs[("dn", g, jt // 4)][:, bs, :])
+                dst = out_1[(jt - 1) * P:(jt + 1) * P, g * W:(g + 1) * W].rearrange("(b p) c -> p b c", b=2)
+                nc.sync.dma_start(out=dst, in_=tile[:])
 
-        def dws(h, k, groups=range(3), role_name="acc"):
+        def dws(h, k, groups=range(3), name="acc"):
             jh, t = divmod(k, 4)
             if groups[0] == 0:
-                acc[("dws", h, k)] = new_bank(role_name)
-            bank = acc[("dws", h, k)]
+                banks[("dws", h, k)] = new_bank(name)
             for g in groups:
-                mm(bank[:], ("b", UNITS.index((h, g))), E5, block(t), ("v", g, jh), E4, slice(0, W), g == 0, g == 2)
+                mm(banks[("dws", h, k)][:], ("b", UNITS.index((h, g))), block(t), ("v", g, jh), slice(0, W), g == 0, g == 2)
 
         def step(h, k):
             jh, t = divmod(k, 4)
-            if t == 0:
-                outs[("step", h, jh)] = out_tile()
+            if t % 2 == 0:
+                outs[("step", h, k // 2)] = out_tile()
+            tile = outs[("step", h, k // 2)]
             nc.scalar.activation(
-                out=outs[("step", h, jh)][:, t, :],
-                in_=acc[("dws", h, k)][:],
+                out=tile[:, t % 2, :],
+                in_=banks[("dws", h, k)][:],
                 func=ACT.Copy,
                 scale=eta32[:, 4 * h + t:4 * h + t + 1],
             )
             if t % 2 == 1:
-                ts = slice(t - 1, t + 1)
-                nc.sync.dma_start(out=rows4(out_2, h, jh)[:, ts, :], in_=outs[("step", h, jh)][:, ts, :])
+                nc.sync.dma_start(out=rows4(out_2, h, jh)[:, t - 1:t + 1, :], in_=tile[:])
 
         gam16 = sb.tile([P, 3, 4], BF16, name="gam16")
         bet16 = sb.tile([P, 3, 4], BF16, name="bet16")
@@ -327,74 +291,63 @@ def tile_gmlp_gating_backward_f3_kernel(tc, dy, wo, u, f, n, gamma, beta, ws, et
         gam = sb.tile([P, 12], F32, name="gam")
         bet = sb.tile([P, 12], F32, name="bet")
         eta32 = sb.tile([P, 8], F32, name="eta32")
-        gam_rows = sb.tile([P, F], BF16, name="gam_rows")
+
+        def widen(dst, src):
+            nc.scalar.activation(out=dst[:], in_=src[:].rearrange("p a b -> p (a b)"), func=ACT.Identity)
+
+        def il_ws(h, jh, engine=nc.scalar):
+            interleave(("ws", h, jh), piece(("ws", h, jh)), engine)
+
+        def il_v(g, jh, engine=nc.scalar):
+            interleave(("v", g, jh), vs[(g, jh)][:], engine)
 
         load_half(("dy", 0), 0, rows4(dy, 0, 0))
         load_half(("wo", 0), 0, wo_rows(0))
         load_half(("dy", 0), 1, rows4(dy, 0, 0))
         nc.scalar.dma_start(out=gam16[:], in_=gamma.rearrange("(g q s) -> q g s", g=3, s=4))
         nc.scalar.dma_start(out=bet16[:], in_=beta.rearrange("(g q s) -> q g s", g=3, s=4))
-        load_half(("wo", 0), 1, wo_rows(0))
         load("u", u, 0, 0, 1)
+        load_half(("wo", 0), 1, wo_rows(0))
         load("f", f, 0, 0, 1)
-        load("n", n, 0, 0, 1)
-        load_wo(1)
-        load("u", u, 0, 1, 2)
-        load("f", f, 0, 1, 2)
-        load_wo(2)
-        nc.sync.dma_start(out=eta16[:], in_=eta.rearrange("(h p t) -> p h t", h=2, t=4))
-        load("n", n, 0, 1, 2)
         load("dy", dy, 1, 0, 1)
+        raw[("dy", 1)] = raw[("dy", 1, 0)]
+        load("ws", ws, 0, 0, 2)
         load("u", u, 1, 0, 1)
         load("f", f, 1, 0, 1)
-        load("ws", ws, 0, 0, 2)
+        load_wo(1)
         load("ws", ws, 1, 0, 2)
+        load("u", u, 0, 1, 2)
+        load("n", n, 0, 0, 1)
+        load("f", f, 0, 1, 2)
+        load_wo(2)
+        load_gamma_rows(0)
+        nc.sync.dma_start(out=eta16[:], in_=eta.rearrange("(h p t) -> p h t", h=2, t=4))
+        load("n", n, 0, 1, 2)
+        load("n", n, 1, 0, 3)
         load("u", u, 1, 1, 2)
         load("f", f, 1, 1, 2)
-        load("n", n, 1, 0, 3)
+        load_gamma_rows(1)
+        load_gamma_rows(2)
 
-        nc.scalar.activation(out=gam[:], in_=gam16[:].rearrange("p g s -> p (g s)"), func=ACT.Identity)
-        turn_half(("dy", 0), 0, "s")
-        turn_half(("wo", 0), 0, "v")
-        quantize(("dy", 0), E4, "dyq", 2, 0, 2)
-        quantize(("wo", 0), E4, "woq", 3, 0, 2)
-        turn_half(("wo", 0), 1, "s")
-        turn_half(("dy", 0), 1, "v")
-        quantize(("wo", 0), E4, "woq", 3, 1, 2)
-        quantize(("dy", 0), E4, "dyq", 2, 1, 2)
-        nc.scalar.activation(out=bet[:], in_=bet16[:].rearrange("p g s -> p (g s)"), func=ACT.Identity)
+        set_banks("dg", (0, 1, 2, 3))
+        set_banks("turn", (4, 5, 6, 7))
+        widen(gam, gam16)
+        turn_rows(("dy", 0), 0)
+        turn_rows(("wo", 0), 0)
+        turn_rows(("dy", 0), 1)
+        turn_rows(("wo", 0), 1)
+        stage_rows(("dy", 0), 0)
+        stage_rows(("wo", 0), 0, nc.vector)
+        stage_rows(("dy", 0), 1)
+        quantize(("dy", 0), 0, 2)
+        quantize(("wo", 0), 0, 2)
+        quantize(("dy", 0), 1, 2)
+        stage_rows(("wo", 0), 1)
+        dg(0)
+        dg(1)
+        widen(bet, bet16)
 
-        def q_dy(h):
-            quantize(("dy", h), E4, "dyq", 2)
-
-        def q_wo(g):
-            quantize(("wo", g), E4, "woq", 3)
-
-        def q_ws(h, jh):
-            quantize(("ws", h, jh), E4, "wsq", 4)
-
-        def q_v(g, jh):
-            quantize(("v", g, jh), E4, "vq", 6)
-
-        def q_a(un):
-            quantize(("a", un), E5, "aq", 5)
-
-        def q_b(un):
-            quantize(("b", un), E5, "bq", 5)
-
-        def il_ws(h, jh):
-            interleave(("ws", h, jh), piece(("ws", h, jh)), WS_ENGINES[2 * jh + h])
-
-        def il_v(g, jh):
-            interleave(("v", g, jh), vs[(g, jh)][:], V_ENGINES[3 * jh + g])
-
-        def eta_f32():
-            nc.scalar.activation(out=eta32[:], in_=eta16[:].rearrange("p h t -> p (h t)"), func=ACT.Identity)
-
-        def narrow_tr():
-            role["tr"] = (3, 4)
-
-        plan = {(i, where): [] for i in range(24) for where in range(4)}
+        plan = {(i, where): [] for i in range(24) for where in range(3)}
 
         def at(i, where, fn, *args):
             plan[(i, where)].append((fn, args))
@@ -403,86 +356,136 @@ def tile_gmlp_gating_backward_f3_kernel(tc, dy, wo, u, f, n, gamma, beta, ws, et
             for fn, args in plan[(i, where)]:
                 fn(*args)
 
-        at(1, 3, turn, ("wo", 1), raw[("wo", 1)])
-        at(2, 3, q_wo, 1)
-        for g in range(3):
-            at(2, 3, spread_gamma, g)
-        at(2, 3, make_v, 0, 0)
-        for un in range(5):
-            at(4 * un + 4, 2, turn_df, un)
-            at(4 * un + 4, 2, il_a, un)
-            at(4 * un + 5, 3, q_a, un)
-            at(4 * un + 6, 3, q_b, un)
-            at(4 * un + 3, 3, store_du, un)
-        at(5, 0, turn, ("wo", 2), raw[("wo", 2)])
-        at(5, 0, il_v, 0, 0)
-        at(6, 3, q_wo, 2)
-        at(6, 3, make_v, 1, 0)
-        at(7, 3, q_v, 0, 0)
-        at(7, 3, il_v, 1, 0)
-        at(8, 3, make_v, 2, 0)
-        at(9, 0, turn, ("dy", 1), raw[("dy", 1, 0)])
-        at(9, 3, q_v, 1, 0)
-        at(9, 3, eta_f32)
-        at(10, 3, q_dy, 1)
-        at(10, 3, il_v, 2, 0)
-        at(12, 3, q_v, 2, 0)
-        at(12, 3, narrow_tr)
-        at(12, 3, il_ws, 0, 0)
-        at(13, 3, il_ws, 1, 0)
-        for k in range(4):
-            at(15, 1, dws, 0, k)
-            at(15, 1, step, 0, k)
-        at(14, 3, q_ws, 0, 0)
-        at(15, 3, q_ws, 1, 0)
-        at(15, 3, il_ws, 0, 1)
-        at(16, 3, il_ws, 1, 1)
-        at(17, 3, q_ws, 0, 1)
-        at(17, 3, make_v, 0, 1)
-        at(18, 3, q_ws, 1, 1)
-        at(18, 3, il_v, 0, 1)
-        at(18, 3, make_v, 1, 1)
-        at(19, 3, il_v, 1, 1)
-        at(19, 3, make_v, 2, 1)
-        at(20, 3, q_v, 0, 1)
-        at(20, 3, il_v, 2, 1)
-        at(21, 3, q_v, 1, 1)
-        at(21, 3, q_v, 2, 1)
+        def pair(i, where, fn, *args):
+            at(i, where, fn, *args, 0)
+            at(i, where, fn, *args, 1)
+
+        Q = quantize
+        du_at = {i: i for i in range(1, 21)}
+
+        def side(i, where, turn, stage, *args):
+            pair(i, where, turn, *args)
+            pair(i, where, stage, *args)
+
+        side(0, 0, turn_rows, stage_rows, ("dy", 1))
+        at(0, 1, Q, ("wo", 0), 1, 2)
+        at(0, 1, dg_rows, 0)
+        at(0, 1, dg_rows, 1)
+        at(0, 1, dg, 2)
+        at(0, 1, il_ws, 0, 0)
+        at(1, 1, dg_rows, 2)
+        at(1, 1, du, 0)
+        at(1, 1, dg, 3)
+        at(1, 2, dg_rows, 3)
+        at(2, 1, Q, ("dy", 1))
+        for i in range(2, 6):
+            at(i, 1, dg, i + 2)
+            at(i, 2, dg_rows, i + 2)
+        at(2, 2, il_ws, 0, 1)
+        side(3, 2, turn_rows, stage_rows, ("wo", 1))
+        at(4, 2, Q, ("a", 0))
+        at(4, 2, il_ws, 1, 0)
+        side(4, 2, turn_df, stage_df, 0)
+        at(5, 2, Q, ("ws", 0, 0))
+        at(6, 1, Q, ("wo", 1))
+        at(6, 1, dg, 8)
+        at(6, 2, set_banks, "dg", (1, 2, 0))
+        at(6, 2, dg, 9)
+        at(6, 2, Q, ("ws", 0, 1))
+        at(7, 1, dg, 10)
+        at(7, 0, il_ws, 1, 1)
+        at(7, 2, Q, ("ws", 1, 0))
+        at(7, 2, set_banks, "turn", (3, 4, 5))
+        at(7, 2, set_banks, "acc", (6, 7))
+        for i in range(9, 22):
+            at(i, 2 if i == 10 else 0, dg, i + 2)
+        at(8, 1, Q, ("a", 1))
+        at(8, 1, dv, 0, 0)
+        side(8, 1, turn_n, make_v, 0, 0)
+        at(8, 2, Q, ("b", 0))
         for jt in range(8):
-            at(17 + jt // 3, 3, dv, 0, jt)
-            at(17 + jt // 3, 3, dn, 0, jt)
+            if jt < 7:
+                at(9 + jt, 0, dv, 0, jt + 1)
+            at(9 + jt, 1, dn, 0, jt)
+        side(9, 0, turn_rows, stage_rows, ("wo", 2))
+        at(9, 2, Q, ("ws", 1, 1))
+        side(10, 0, turn_df, stage_df, 1)
+        at(10, 1, Q, ("wo", 2))
+        at(10, 2, il_v, 0, 0, nc.vector)
+        side(11, 0, turn_n, make_v, 1, 0)
+        at(11, 2, Q, ("v", 0, 0))
+        at(11, 2, Q, ("b", 1))
+        side(11, 2, turn_n, make_v, 2, 0)
+        at(11, 2, il_v, 2, 0)
+        at(12, 2, il_v, 1, 0, nc.vector)
+        side(12, 1, turn_df, stage_df, 2)
+        at(13, 2, Q, ("v", 1, 0))
+        at(13, 2, Q, ("a", 2))
+        side(13, 1, turn_n, make_v, 0, 1)
+        at(14, 2, Q, ("v", 2, 0))
+        at(14, 2, Q, ("b", 2))
+        side(15, 1, turn_df, stage_df, 3)
+        at(14, 0, il_v, 0, 1)
+        at(14, 0, widen, eta32, eta16)
+        at(15, 2, dws, 0, 0, range(2))
+        side(16, 0, turn_n, make_v, 1, 1)
+        at(16, 1, dws, 0, 1, range(2))
+        at(17, 1, Q, ("b", 3))
+        at(16, 2, set_banks, "turn", (3, 4))
+        at(16, 2, set_banks, "acc", (5, 6, 7))
+        at(16, 2, dws, 0, 2, range(2))
+        for k in range(3):
+            at(17, 1, dws, 0, k, range(2, 3))
+            at(17, 1, step, 0, k)
+        at(17, 1, dws, 0, 3)
+        at(17, 1, step, 0, 3)
+        side(18, 0, turn_n, make_v, 2, 1)
+        at(16, 2, Q, ("v", 0, 1))
+        at(19, 0, il_v, 2, 1)
+        at(19, 2, Q, ("a", 4))
+        for jt in range(3):
+            at(19, 2, dv, 1, jt)
+        at(19, 2, il_v, 1, 1, nc.vector)
+        side(20, 2, turn_df, stage_df, 4)
+        at(20, 1, Q, ("v", 1, 1))
         for jt in range(8):
-            at(21, 3, dv, 1, jt)
-            at(21, 3, dn, 1, jt)
+            at(20 + jt // 6, 2 - jt // 6 * 2, dn, 1, jt)
+            if jt < 5:
+                at(20, 2, dv, 1, jt + 3)
+        at(20, 2, Q, ("v", 2, 1))
+        at(21, 0, Q, ("b", 4))
         for k in range(4, 8):
-            at(21, 3, dws, 0, k)
-            at(21, 3, step, 0, k)
+            at(21, 0, dws, 0, k)
+            at(21, 0, step, 0, k)
 
         for i in range(24):
             run(i, 0)
-            dg(i)
-            run(i, 1)
             df(i)
+            run(i, 1)
+            if i in du_at:
+                du(du_at[i])
             run(i, 2)
-            if i < 23:
-                du(i)
-            run(i, 3)
 
-        turn_df(5)
-        il_a(5)
-        du(23)
-        store_du(5)
-        q_a(5)
-        q_b(5)
+        for w in range(2):
+            turn_df(5, w)
+            stage_df(5, w)
+        quantize(("a", 3))
+        quantize(("a", 5))
         for k in range(3):
             dws(1, k, range(2))
-        role["tail"] = (0, 1, 2, 3, 4)
+        set_banks("tail", (1, 2, 0, 3, 4))
+        for jt in range(3):
+            du(21 + jt)
+            dv(2, jt, range(2), "tail")
+        quantize(("b", 5))
+        dv(2, 3, range(2), "tail")
+        dv(2, 4, range(2), "tail")
         for jt in range(8):
-            dv(2, jt, "tail")
             dn(2, jt)
-            if jt in (1, 3, 5):
-                dws(1, jt // 2, range(2, 3))
-                step(1, jt // 2)
+            if jt < 3:
+                dv(2, jt + 5, range(2), "tail")
+                dws(1, jt, range(2, 3))
+                step(1, jt)
         for k in range(3, 8):
             dws(1, k)
             step(1, k)

from contextlib import ExitStack

import concourse.mybir as mybir
from concourse.masks import make_identity

T, D, F = 1024, 512, 1536
FLOPS = 2 * T * D * F + 4 * T * T * F

F32 = mybir.dt.float32
BF16 = mybir.dt.bfloat16
U32 = mybir.dt.uint32
U8 = mybir.dt.uint8
E4 = mybir.dt.float8_e4m3fn_x4
E5 = mybir.dt.float8_e5m2_x4
ACT = mybir.ActivationFunctionType
MULT = mybir.AluOpType.mult

P = 128
W = 512
UNITS = [(0, 0), (1, 0), (0, 1), (0, 2), (1, 1), (1, 2)]
OWN_PASS = (0, 1)
LATE_DU = 20


def tile_gmlp_gating_backward_f3_kernel(tc, dy, wo, u, f, n, gamma, beta, ws, eta, out_0, out_1, out_2):
    nc = tc.nc
    with ExitStack() as ctx:
        sb = ctx.enter_context(tc.tile_pool(name="sb", bufs=1))
        ps = ctx.enter_context(tc.psum_pool(name="ps", bufs=1))
        turns = {}

        def rotate(pool, tags, shape, dtype, **kw):
            k = turns.get(tags, 0)
            turns[tags] = k + 1
            tag = tags[k % len(tags)]
            return pool.tile(shape, dtype, name=tag, tag=tag, **kw)

        def slot(tag, shape, dtype):
            return sb.tile(shape, dtype, name=tag, tag=tag, align_bytes=64)

        def ring(name, slots, shape, dtype):
            return rotate(sb, tuple("%s%d" % (name, k) for k in range(slots)), shape, dtype, align_bytes=64)

        out_tags = ("out0", "out1", "out2", "out3", "u_one0", "f_one0", "dy_one1", "u_one1", "f_one1", "wo1", "ws_wide0", "ws_wide1", "n_one0")

        def out_tile():
            return rotate(sb, out_tags, [P, 2, W], F32, align_bytes=64)

        role = {}

        def set_banks(name, banks):
            role[name] = tuple("bank%d" % b for b in banks)

        def new_bank(name):
            return rotate(ps, role[name], [P, W], F32)

        ident = sb.tile([P, P], F32, name="ident")
        make_identity(nc, ident[:])

        raw = {}

        def rows4(x, h, g, groups=1):
            return x[h * W:(h + 1) * W, g * W:(g + groups) * W].rearrange("(p t) c -> p t c", t=4)

        def load(name, x, h, g, groups):
            tile = slot("%s_%s%d" % (name, "wide" if groups > 1 else "one", h), [P, 4, groups * W], BF16)
            nc.sync.dma_start(out=tile[:], in_=rows4(x, h, g, groups))
            for j in range(groups):
                raw[(name, h, g + j)] = (tile, j)

        def piece(key):
            tile, j = raw[key]
            return tile[:, :, j * W:(j + 1) * W]

        def word_columns(key, a, w):
            tile, j = raw[key]
            base = a * tile.shape[2] // 2 + j * 256
            return tile[:].rearrange("p a c -> p (a c)").bitcast(F32)[:, base + w:base + 256:2]

        def wo_rows(g):
            return wo[g * W:(g + 1) * W, :].rearrange("(b m) k -> m b k", b=4)

        def load_wo(g):
            tile = slot("wo%d" % g, [P, 4, W], BF16)
            nc.sync.dma_start(out=tile[:], in_=wo_rows(g))
            raw[("wo", g)] = (tile, 0)

        def load_half(key, half, src):
            tile = ring("first", 4, [P, 2, W], BF16)
            nc.sync.dma_start(out=tile[:], in_=src[:, 2 * half:2 * half + 2, :])
            raw[key + (half,)] = (tile, 0)

        codes = {}
        staged = {}
        banks = {}
        formats = {"dy": (E4, 2), "wo": (E4, 3), "ws": (E4, 4), "v": (E4, 6), "a": (E5, 4), "b": (E5, 5)}

        def quantize(key, part=0, parts=1):
            fmt, slots = formats[key[0]]
            if part == 0:
                codes[key] = (ring(key[0] + "_codes", slots, [P, W], U32), ring(key[0] + "_scales", slots, [P, W], U8))
            width = W // parts
            cols = slice(part * width, (part + 1) * width)
            nc.vector.quantize_mx(
                out=codes[key][0][:, cols].bitcast(fmt),
                scales=codes[key][1][:, cols],
                in_=staged[key][:, 4 * part * width:4 * (part + 1) * width],
            )

        def mm(bank, lhs, lhs_cols, rhs, rhs_cols, start, stop):
            nc.tensor.matmul_mx(
                out=bank,
                lhsT=codes[lhs][0][:, lhs_cols].bitcast(formats[lhs[0]][0]),
                lhsT_scale=codes[lhs][1][:, lhs_cols],
                rhs=codes[rhs][0][:, rhs_cols].bitcast(formats[rhs[0]][0]),
                rhs_scale=codes[rhs][1][:, rhs_cols],
                start=start,
                stop=stop,
            )

        def block(j):
            return slice(j * P, (j + 1) * P)

        def new_staged(key):
            staged[key] = ring("staged", 7, [P, 4 * W], BF16)

        def copy_on(engine, out, in_):
            if engine is nc.scalar:
                nc.scalar.copy(out=out, in_=in_)
            else:
                nc.vector.tensor_copy(out=out, in_=in_)

        def turn_rows(key, half):
            bank = new_bank("turn")
            banks[key + (half,)] = bank
            for a in range(2):
                for w in range(2):
                    if key in raw:
                        cols = word_columns(key, 2 * half + a, w)
                    else:
                        cols = word_columns(key + (half,), a, w)
                    nc.tensor.transpose(bank[:, block(2 * a + w)], cols, ident[:])

        def stage_rows(key, half, engine=nc.scalar):
            if half == 0:
                new_staged(key)
            out = staged[key][:].bitcast(F32)[:, half * W:(half + 1) * W].rearrange("p (a m w) -> p a m w", a=2, w=2)
            copy_on(engine, out, banks[key + (half,)][:].rearrange("p (a w m) -> p a m w", a=2, w=2))

        def interleave(key, src, engine):
            new_staged(key)
            copy_on(engine, staged[key][:].rearrange("p (c i t) -> p c t i", i=4, t=4), src.rearrange("p t (c i) -> p c t i", i=4))

        outs = {}

        def dg(i):
            h, g = UNITS[i // 4]
            bank = new_bank("dg")
            banks[("df", i)] = bank
            for t in range(4):
                mm(bank[:, block(t)], ("dy", h), block(t), ("wo", g), block(i % 4), True, True)

        def dg_rows(i, name="dg"):
            h, g = UNITS[i // 4]
            bank = new_bank(name)
            banks[("du", i)] = bank
            mm(bank[:], ("dy", h), block(i % 4), ("wo", g), slice(0, W), True, True)

        def df(i):
            un, b = divmod(i, 4)
            if b == 0:
                staged[("a", un)] = ring("df", 3, [P, 4 * W], BF16)
            nc.vector.tensor_tensor(
                out=staged[("a", un)][:].rearrange("p (s q t) -> p q t s", s=4, t=4)[:, 32 * b:32 * (b + 1), :, :],
                in0=banks[("df", i)][:].rearrange("p (t q s) -> p q t s", t=4, s=4),
                in1=piece(("u",) + UNITS[un])[:, :, block(b)].rearrange("p t (q s) -> p q t s", s=4),
                op=MULT,
            )

        def du(i):
            un, b = divmod(i, 4)
            h, g = UNITS[un]
            if un in OWN_PASS:
                if b % 2 == 0:
                    outs[("du", i // 2)] = out_tile()
                tile = outs[("du", i // 2)]
                nc.vector.tensor_tensor(out=tile[:, b % 2, :], in0=banks[("du", i)][:], in1=piece(("f", h, g))[:, b, :], op=MULT)
                if b % 2 == 1:
                    nc.sync.dma_start(out=rows4(out_0, h, g)[:, b - 1:b + 1, :], in_=tile[:])
            else:
                if b % 2 == 0:
                    outs[("du", i // 2)] = out_tile()
                tile = outs[("du", i // 2)][:].rearrange("p a c -> p (a c)").rearrange("p (t c) -> p t c", t=4)
                nc.vector.tensor_tensor(
                    out=tile[:, :, block(b % 2)],
                    in0=banks[("df", i)][:].rearrange("p (t c) -> p t c", t=4),
                    in1=piece(("f", h, g))[:, :, block(b)],
                    op=MULT,
                )
                if b % 2 == 1:
                    nc.sync.dma_start(out=rows4(out_0, h, g)[:, :, (b - 1) * P:(b + 1) * P], in_=tile)

        def turn_df(un, w):
            bank = new_bank("turn")
            banks[("b", un, w)] = bank
            words = staged[("a", un)][:].bitcast(F32)
            for s in range(4):
                nc.tensor.transpose(bank[:, block(s)], words[:, 256 * s + w:256 * (s + 1):2], ident[:])

        def stage_df(un, w, engine=nc.scalar):
            if w == 0:
                new_staged(("b", un))
            copy_on(
                engine,
                staged[("b", un)][:, w * 2 * W:(w + 1) * 2 * W].rearrange("p (e m s) -> p e m s", e=2, s=4),
                banks[("b", un, w)][:].bitcast(BF16).rearrange("p (s m e) -> p e m s", s=4, e=2),
            )

        vs = {}

        def turn_n(g, jh, w):
            bank = new_bank("turn")
            banks[("n", g, jh, w)] = bank
            for a in range(4):
                nc.tensor.transpose(bank[:, block(a)], word_columns(("n", jh, g), a, w), ident[:])

        def make_v(g, jh, w):
            if w == 0:
                vs[(g, jh)] = ring("v_rows", 2, [P, 4, W], BF16)
            halves = banks[("n", g, jh, w)][:].bitcast(BF16).rearrange("p (a m e) -> p e m a", a=4, e=2)
            for e in range(2):
                s = 2 * w + e
                nc.scalar.activation(
                    out=vs[(g, jh)][:, s, :].rearrange("p (m a) -> p m a", a=4),
                    in_=halves[:, e, :, :],
                    func=ACT.Identity,
                    scale=gam[:, 4 * g + s:4 * g + s + 1],
                    bias=bet[:, 4 * g + s:4 * g + s + 1],
                )

        gam_rows = {}

        def load_gamma_rows(g):
            gam_rows[g] = slot("gamma_rows%d" % g, [P, W], BF16)
            nc.sync.dma_start(out=gam_rows[g][:], in_=gamma[g * W:(g + 1) * W].partition_broadcast(P))

        def dv(g, jt, halves=range(2), name="acc"):
            if halves[0] == 0:
                banks[("dv", g, jt)] = new_bank(name)
            for h in halves:
                mm(banks[("dv", g, jt)][:], ("ws", h, jt // 4), block(jt % 4), ("a", UNITS.index((h, g))), slice(0, W), h == 0, h == 1)

        def dn(g, jt):
            if jt % 2 == 0:
                outs[("dn", g, jt // 2)] = out_tile()
            tile = outs[("dn", g, jt // 2)]
            nc.vector.tensor_tensor(
                out=tile[:, jt % 2, :].rearrange("p (q s) -> p q s", s=4),
                in0=banks[("dv", g, jt)][:].rearrange("p (s q) -> p q s", s=4),
                in1=gam_rows[g][:].rearrange("p (q s) -> p q s", s=4),
                op=MULT,
            )
            if jt % 2 == 1:
                dst = out_1[(jt - 1) * P:(jt + 1) * P, g * W:(g + 1) * W].rearrange("(b p) c -> p b c", b=2)
                nc.sync.dma_start(out=dst, in_=tile[:])

        def dws(h, k, groups=range(3), name="acc"):
            jh, t = divmod(k, 4)
            if groups[0] == 0:
                banks[("dws", h, k)] = new_bank(name)
            for g in groups:
                mm(banks[("dws", h, k)][:], ("b", UNITS.index((h, g))), block(t), ("v", g, jh), slice(0, W), g == 0, g == 2)

        def step(h, k):
            jh, t = divmod(k, 4)
            if t % 2 == 0:
                outs[("step", h, k // 2)] = out_tile()
            tile = outs[("step", h, k // 2)]
            nc.scalar.activation(
                out=tile[:, t % 2, :],
                in_=banks[("dws", h, k)][:],
                func=ACT.Copy,
                scale=eta32[:, 4 * h + t:4 * h + t + 1],
            )
            if t % 2 == 1:
                nc.sync.dma_start(out=rows4(out_2, h, jh)[:, t - 1:t + 1, :], in_=tile[:])

        gam16 = sb.tile([P, 3, 4], BF16, name="gam16")
        bet16 = sb.tile([P, 3, 4], BF16, name="bet16")
        eta16 = sb.tile([P, 2, 4], BF16, name="eta16")
        gam = sb.tile([P, 12], F32, name="gam")
        bet = sb.tile([P, 12], F32, name="bet")
        eta32 = sb.tile([P, 8], F32, name="eta32")

        def widen(dst, src):
            nc.scalar.activation(out=dst[:], in_=src[:].rearrange("p a b -> p (a b)"), func=ACT.Identity)

        def il_ws(h, jh, engine=nc.scalar):
            interleave(("ws", h, jh), piece(("ws", h, jh)), engine)

        def il_v(g, jh, engine=nc.scalar):
            interleave(("v", g, jh), vs[(g, jh)][:], engine)

        load_half(("dy", 0), 0, rows4(dy, 0, 0))
        load_half(("wo", 0), 0, wo_rows(0))
        load_half(("dy", 0), 1, rows4(dy, 0, 0))
        nc.scalar.dma_start(out=gam16[:], in_=gamma.rearrange("(g q s) -> q g s", g=3, s=4))
        nc.scalar.dma_start(out=bet16[:], in_=beta.rearrange("(g q s) -> q g s", g=3, s=4))
        load("u", u, 0, 0, 1)
        load_half(("wo", 0), 1, wo_rows(0))
        load("f", f, 0, 0, 1)
        load("dy", dy, 1, 0, 1)
        raw[("dy", 1)] = raw[("dy", 1, 0)]
        load("ws", ws, 0, 0, 2)
        load("u", u, 1, 0, 1)
        load("f", f, 1, 0, 1)
        load_wo(1)
        load("ws", ws, 1, 0, 2)
        load("u", u, 0, 1, 2)
        load("n", n, 0, 0, 1)
        load("f", f, 0, 1, 2)
        load_wo(2)
        load_gamma_rows(0)
        nc.sync.dma_start(out=eta16[:], in_=eta.rearrange("(h p t) -> p h t", h=2, t=4))
        load("n", n, 0, 1, 2)
        load("n", n, 1, 0, 3)
        load("u", u, 1, 1, 2)
        load("f", f, 1, 1, 2)
        load_gamma_rows(1)
        load_gamma_rows(2)

        set_banks("dg", (0, 1, 2, 3))
        set_banks("turn", (4, 5, 6, 7))
        widen(gam, gam16)
        turn_rows(("dy", 0), 0)
        turn_rows(("wo", 0), 0)
        turn_rows(("dy", 0), 1)
        turn_rows(("wo", 0), 1)
        stage_rows(("dy", 0), 0)
        stage_rows(("wo", 0), 0, nc.vector)
        stage_rows(("dy", 0), 1)
        quantize(("dy", 0), 0, 2)
        quantize(("wo", 0), 0, 2)
        quantize(("dy", 0), 1, 2)
        stage_rows(("wo", 0), 1)
        dg(0)
        dg(1)
        widen(bet, bet16)

        plan = {(i, where): [] for i in range(24) for where in range(3)}

        def at(i, where, fn, *args):
            plan[(i, where)].append((fn, args))

        def run(i, where):
            for fn, args in plan[(i, where)]:
                fn(*args)

        def pair(i, where, fn, *args):
            at(i, where, fn, *args, 0)
            at(i, where, fn, *args, 1)

        Q = quantize
        du_at = {i: i for i in range(1, 21)}

        def side(i, where, turn, stage, *args):
            pair(i, where, turn, *args)
            pair(i, where, stage, *args)

        side(0, 0, turn_rows, stage_rows, ("dy", 1))
        at(0, 1, Q, ("wo", 0), 1, 2)
        at(0, 1, dg_rows, 0)
        at(0, 1, dg_rows, 1)
        at(0, 1, dg, 2)
        at(0, 1, il_ws, 0, 0)
        at(1, 1, dg_rows, 2)
        at(1, 1, du, 0)
        at(1, 1, dg, 3)
        at(1, 2, dg_rows, 3)
        at(2, 1, Q, ("dy", 1))
        for i in range(2, 6):
            at(i, 1, dg, i + 2)
            at(i, 2, dg_rows, i + 2)
        at(2, 2, il_ws, 0, 1)
        side(3, 2, turn_rows, stage_rows, ("wo", 1))
        at(4, 2, Q, ("a", 0))
        at(4, 2, il_ws, 1, 0)
        side(4, 2, turn_df, stage_df, 0)
        at(5, 2, Q, ("ws", 0, 0))
        at(6, 1, Q, ("wo", 1))
        at(6, 1, dg, 8)
        at(6, 2, set_banks, "dg", (1, 2, 0))
        at(6, 2, dg, 9)
        at(6, 2, Q, ("ws", 0, 1))
        at(7, 1, dg, 10)
        at(7, 0, il_ws, 1, 1)
        at(7, 2, Q, ("ws", 1, 0))
        at(7, 2, set_banks, "turn", (3, 4, 5))
        at(7, 2, set_banks, "acc", (6, 7))
        for i in range(9, 22):
            at(i, 2 if i == 10 else 0, dg, i + 2)
        at(8, 1, Q, ("a", 1))
        at(8, 1, dv, 0, 0)
        side(8, 1, turn_n, make_v, 0, 0)
        at(8, 2, Q, ("b", 0))
        for jt in range(8):
            if jt < 7:
                at(9 + jt, 0, dv, 0, jt + 1)
            at(9 + jt, 1, dn, 0, jt)
        side(9, 0, turn_rows, stage_rows, ("wo", 2))
        at(9, 2, Q, ("ws", 1, 1))
        side(10, 0, turn_df, stage_df, 1)
        at(10, 1, Q, ("wo", 2))
        at(10, 2, il_v, 0, 0, nc.vector)
        side(11, 0, turn_n, make_v, 1, 0)
        at(11, 2, Q, ("v", 0, 0))
        at(11, 2, Q, ("b", 1))
        side(11, 2, turn_n, make_v, 2, 0)
        at(11, 2, il_v, 2, 0)
        at(12, 2, il_v, 1, 0, nc.vector)
        side(12, 1, turn_df, stage_df, 2)
        at(13, 2, Q, ("v", 1, 0))
        at(13, 2, Q, ("a", 2))
        side(13, 1, turn_n, make_v, 0, 1)
        at(14, 2, Q, ("v", 2, 0))
        at(14, 2, Q, ("b", 2))
        side(15, 1, turn_df, stage_df, 3)
        at(14, 0, il_v, 0, 1)
        at(14, 0, widen, eta32, eta16)
        at(15, 2, dws, 0, 0, range(2))
        side(16, 0, turn_n, make_v, 1, 1)
        at(16, 1, dws, 0, 1, range(2))
        at(17, 1, Q, ("b", 3))
        at(16, 2, set_banks, "turn", (3, 4))
        at(16, 2, set_banks, "acc", (5, 6, 7))
        at(16, 2, dws, 0, 2, range(2))
        for k in range(3):
            at(17, 1, dws, 0, k, range(2, 3))
            at(17, 1, step, 0, k)
        at(17, 1, dws, 0, 3)
        at(17, 1, step, 0, 3)
        side(18, 0, turn_n, make_v, 2, 1)
        at(16, 2, Q, ("v", 0, 1))
        at(19, 0, il_v, 2, 1)
        at(19, 2, Q, ("a", 4))
        for jt in range(3):
            at(19, 2, dv, 1, jt)
        at(19, 2, il_v, 1, 1, nc.vector)
        side(20, 2, turn_df, stage_df, 4)
        at(20, 1, Q, ("v", 1, 1))
        for jt in range(8):
            at(20 + jt // 6, 2 - jt // 6 * 2, dn, 1, jt)
            if jt < 5:
                at(20, 2, dv, 1, jt + 3)
        at(20, 2, Q, ("v", 2, 1))
        at(21, 0, Q, ("b", 4))
        for k in range(4, 8):
            at(21, 0, dws, 0, k)
            at(21, 0, step, 0, k)

        for i in range(24):
            run(i, 0)
            df(i)
            run(i, 1)
            if i in du_at:
                du(du_at[i])
            run(i, 2)

        for w in range(2):
            turn_df(5, w)
            stage_df(5, w)
        quantize(("a", 3))
        quantize(("a", 5))
        for k in range(3):
            dws(1, k, range(2))
        set_banks("tail", (1, 2, 0, 3, 4))
        for jt in range(3):
            du(21 + jt)
            dv(2, jt, range(2), "tail")
        quantize(("b", 5))
        dv(2, 3, range(2), "tail")
        dv(2, 4, range(2), "tail")
        for jt in range(8):
            dn(2, jt)
            if jt < 3:
                dv(2, jt + 5, range(2), "tail")
                dws(1, jt, range(2, 3))
                step(1, jt)
        for k in range(3, 8):
            dws(1, k)
            step(1, k)
